import numpy as np
import ml_dtypes


def mxq(x, axis, fmt="e4m3"):
    dtype, down = {"e4m3": (ml_dtypes.float8_e4m3fn, 7), "e5m2": (ml_dtypes.float8_e5m2, 14)}[fmt]
    v = np.moveaxis(np.asarray(x, np.float32).astype(ml_dtypes.bfloat16).astype(np.float64), axis, -1)
    blocks = v.reshape(v.shape[:-1] + (-1, 32))
    amax = np.abs(blocks).max(-1, keepdims=True)
    byte = np.maximum(np.where(amax > 0, np.frexp(amax)[1] - 1 + 127, 0) - down, 1)
    scale = np.exp2(byte - 127.0)
    codes = (blocks / scale).astype(np.float32).astype(dtype).astype(np.float64)
    return np.moveaxis((codes * scale).reshape(v.shape), -1, axis)


WIDE = False


def mx_kscale(k):
    if not WIDE:
        return np.ones(k)
    levels = np.array([10, -10, 5, -5, 0])
    if k % 512:
        return np.exp2(np.random.permutation(np.resize(levels, k // 32))).repeat(32)
    a = np.empty((k // 512, 16))
    for p in range(k // 512):
        a[p, :8] = np.random.permutation(np.resize(levels, 8))
        for g in range(8):
            far = levels[np.abs(levels - a[p, g]) >= 10]
            a[p, g + 8] = far[np.random.randint(len(far))]
    return np.exp2(a.ravel()).repeat(32)


def f64(x):
    return np.asarray(x).astype(np.float64)


def striped(idx):
    return np.tile(idx.reshape(-1, 16).T, (8, 1)).astype(np.uint16)


def unstriped(offs):
    return offs[:16].T.reshape(-1).astype(np.int64)


E2M1 = np.array([0.0, 0.5, 1.0, 1.5, 2.0, 3.0, 4.0, 6.0, -0.0, -0.5, -1.0, -1.5, -2.0, -3.0, -4.0, -6.0])


def pack_weight(w, fmt):
    k, n = w.shape
    w = f64(np.asarray(w, np.float32).astype(ml_dtypes.bfloat16)).reshape(k // 32, 32, n)
    amax = np.abs(w).max(1)
    if fmt == "e4m3":
        byte = np.frexp(amax)[1] - 1 + 127 - 7
    else:
        mant, ex = np.frexp(amax / 6.0)
        byte = np.where(mant > 0.5, ex, ex - 1) + 127
    byte = np.clip(np.where(amax > 0, byte, 1), 1, 254)
    scaled = (w * np.exp2(127.0 - byte)[:, None, :]).reshape(k, n).astype(np.float32)
    by_word = np.ascontiguousarray(scaled.reshape(k // 512, 128, 4, n).transpose(0, 1, 3, 2))
    if fmt == "e4m3":
        words = by_word.astype(ml_dtypes.float8_e4m3fn).view(np.uint8)
    else:
        c = by_word.astype(ml_dtypes.float4_e2m1fn).view(np.uint8) & 0xF
        words = (c[..., 0::2] | (c[..., 1::2] << 4)).reshape(k // 512, 128, 2 * n)
    return np.ascontiguousarray(words), np.ascontiguousarray(byte.astype(np.uint8).reshape(k // 512, 16, n))


def unpack_weight(words, scales, fmt):
    g, _, n = scales.shape
    words = np.ascontiguousarray(words).reshape(g, 128, n, -1)
    if fmt == "e4m3":
        vals = words.view(ml_dtypes.float8_e4m3fn).astype(np.float64)
    else:
        nib = np.empty((g, 128, n, 4), np.uint8)
        nib[..., 0::2] = words & 0xF
        nib[..., 1::2] = words >> 4
        vals = E2M1[nib]
    vals = vals * np.repeat(np.exp2(scales.astype(np.float64) - 127.0), 8, axis=1)[..., None]
    return vals.transpose(0, 1, 3, 2).reshape(g * 512, n)


def gelu(v):
    return 0.5 * v * (1.0 + np.tanh(np.sqrt(2.0 / np.pi) * (v + 0.044715 * v**3)))


K, T, S, M, N = 1024, 2048, 1024, 512, 512


def setup_inputs():
    n = np.random.standard_normal
    s = mx_kscale(K)[:, None]
    u = mx_kscale(S)
    idx = np.random.permutation(T)[:S]
    tab_words, tab_scales = pack_weight(n((K, T)) / np.sqrt(K) * s, "e4m3")
    x = n((K, M)) / s
    xn_words, xn_scales = pack_weight(n((K, M)) / s, "e2m1")
    g = np.exp(0.3 * n(S)) * u
    wdT = n((N, T)) / np.sqrt(S)
    wdT[:, idx] /= u
    gam = np.random.uniform(0.6, 0.99, M)
    return {"tab_words": tab_words, "tab_scales": tab_scales, "offs": striped(idx),
            "x": x.astype(np.float32), "xn_words": xn_words, "xn_scales": xn_scales,
            "g": g.astype(np.float32), "wdT": wdT.astype(np.float32),
            "gam": gam.astype(np.float32)}


def reference(tab_words, tab_scales, offs, x, xn_words, xn_scales, g, wdT, gam):
    v = unpack_weight(tab_words, tab_scales, "e4m3")[:, unstriped(offs)]
    xq = mxq(f64(x), 0, "e4m3")
    xn = unpack_weight(xn_words, xn_scales, "e2m1")
    p = np.concatenate([(v.T @ xq), (v.T @ xn)], axis=1)
    h = np.maximum(p, 0.0) * f64(g)[:, None]
    hq = mxq(h, 0, "e4m3")
    wd = f64(wdT)[:, unstriped(offs)]
    y = mxq(wd, 1, "e4m3") @ hq
    return f64(gam)[None, :] * y[:, M:] - y[:, :M]

@@ -1,0 +1,232 @@
+from contextlib import ExitStack
+
+import concourse.mybir as mybir
+from concourse.masks import make_identity
+
+K, T, S, M, N = 1024, 2048, 1024, 512, 512
+FLOPS = 2 * K * S * 2 * M + 2 * S * N * 2 * M
+
+F32 = mybir.dt.float32
+BF16 = mybir.dt.bfloat16
+I32 = mybir.dt.int32
+U32 = mybir.dt.uint32
+U16 = mybir.dt.uint16
+U8 = mybir.dt.uint8
+FP8X4 = mybir.dt.float8_e4m3fn_x4
+FP4X4 = mybir.dt.float4_e2m1fn_x4
+ALU = mybir.AluOpType
+ACT = mybir.ActivationFunctionType
+
+P = 128
+
+
+def tile_list_sparse_td_features_kernel(tc, tab_words, tab_scales, offs, x, xn_words, xn_scales, g, wdT, gam, out):
+    nc = tc.nc
+    with ExitStack() as ctx:
+        keep = ctx.enter_context(tc.tile_pool(name="keep", bufs=1))
+        ring = ctx.enter_context(tc.tile_pool(name="ring", bufs=2))
+        psum = ctx.enter_context(tc.psum_pool(name="psum", bufs=1))
+
+        offsets = keep.tile([P, S // 16], U16, name="offsets")
+        tab_s = keep.tile([P, T], U8, name="tab_s", align_bytes=64)
+        tab_w = [keep.tile([P, T], U32, name="tab_w%d" % a, align_bytes=64) for a in range(2)]
+        xn_w = keep.tile([P, 2, 2 * M], U8, name="xn_w", align_bytes=64)
+        xn_s = keep.tile([P, 2, M], U8, name="xn_s", align_bytes=64)
+        v_s_listed = keep.tile([P, S], U8, name="v_s_listed", align_bytes=64)
+        v_s = keep.tile([P, 8, P], U8, name="v_s", align_bytes=64)
+        v_s1 = keep.tile([P, 8, P], U8, name="v_s1", align_bytes=64)
+        v_w = [keep.tile([P, 8, P], U32, name="v_w%d" % a, align_bytes=64) for a in range(2)]
+        x_raw = [keep.tile([P, 4, M], F32, name="x_raw%d" % a) for a in range(2)]
+        wd_raw = [keep.tile([P, T], F32, name="wd_raw%d" % i) for i in range(4)]
+        rows = keep.tile([P, P], F32, name="rows")
+        ident = keep.tile([P, P], F32, name="ident")
+
+        nc.vector.memset(tab_s[:].bitcast(I32), 0)
+        nc.vector.memset(rows[:], 0.0)
+        nc.vector.memset(xn_s[:].rearrange("p a c -> p (a c)").bitcast(I32), 0)
+        nc.vector.memset(v_s1[:].rearrange("p t c -> p (t c)").bitcast(I32), 0)
+        make_identity(nc, ident[:])
+
+        nc.sync.dma_start(offsets[:], offs)
+        for q in range(4):
+            nc.sync.dma_start(tab_s[32 * q : 32 * q + 8, :].bitcast(I32), tab_scales[:, 4 * q : 4 * q + 4, :].bitcast(I32))
+        for a in range(2):
+            nc.sync.dma_start(tab_w[a][:].bitcast(I32), tab_words[a].rearrange("p t i -> p (t i)").bitcast(I32))
+        nc.sync.dma_start(xn_w[:].bitcast(I32), xn_words.rearrange("a p c -> p a c").bitcast(I32))
+        nc.scalar.dma_start(rows[0:8, :].rearrange("s (q r) -> s q r", r=8), g.rearrange("(q s r) -> s q r", s=8, r=8))
+        nc.scalar.dma_start(rows[8:12, :], gam.rearrange("(c p) -> c p", p=P))
+        for q in range(4):
+            nc.gpsimd.dma_start(xn_s[32 * q : 32 * q + 4, :, :].bitcast(I32), xn_scales[:, 4 * q : 4 * q + 4, :].rearrange("a r c -> r a c").bitcast(I32))
+
+        def load_wd(i):
+            nc.sync.dma_start(wd_raw[i][:], wdT[P * i : P * (i + 1), :])
+
+        def load_x(a):
+            nc.sync.dma_start(x_raw[a][:], x[512 * a : 512 * (a + 1), :].rearrange("(p j) m -> p j m", j=4))
+
+        load_wd(0)
+        load_x(1)
+        load_x(0)
+        for i in range(1, 4):
+            load_wd(i)
+
+        nc.vector.tensor_copy(v_s_listed[:], tab_s[:].indirect(offsets[:]))
+        nc.vector.tensor_copy(
+            v_s[:].bitcast(I32).rearrange("p s (q w) -> p s q w", w=2),
+            v_s_listed[:].bitcast(I32).rearrange("p (q s w) -> p s q w", s=8, w=2),
+        )
+        nc.gpsimd.dma_start(
+            v_s1[0:112, :, :].rearrange("p t c -> p (t c)").bitcast(I32),
+            v_s[4:116, :, :].rearrange("p t c -> p (t c)").bitcast(I32),
+        )
+        for a in range(2):
+            nc.vector.tensor_copy(v_w[a][:].rearrange("p s (q r) -> p q s r", r=8), tab_w[a][:].indirect(offsets[:]))
+
+        cols_ps = psum.tile([P, P], F32, name="cols_ps", tag="tr", bufs=2)
+        nc.tensor.transpose(cols_ps[:], rows[:], ident[:])
+        gain = keep.tile([P, 8], F32, name="gain")
+        sign0 = keep.tile([P, 8], F32, name="sign0")
+        sign = keep.tile([P, 8], BF16, name="sign")
+        gam_cols = keep.tile([P, 4], F32, name="gam_cols")
+        nc.scalar.activation(gain[:], cols_ps[:, 0:8], ACT.Abs)
+        nc.scalar.activation(sign0[:], cols_ps[:, 0:8], ACT.Sign)
+        nc.scalar.copy(gam_cols[:], cols_ps[:, 8:12])
+        nc.scalar.activation(sign[:], sign0[:], ACT.Sign, bias=0.5)
+        gam_row = keep.tile([P, M], F32, name="gam_row")
+        spread = psum.tile([P, 4, P], F32, name="spread", tag="y", bufs=3)
+        for c in range(4):
+            nc.tensor.transpose(spread[:, c, :], gam_cols[:, c : c + 1].to_broadcast([P, P]), ident[:])
+        nc.scalar.copy(gam_row[:], spread[:].rearrange("p c m -> p (c m)"))
+
+        x_w = [keep.tile([P, M], U32, name="x_w%d" % a, align_bytes=64) for a in range(2)]
+        x_s = [keep.tile([P, M], U8, name="x_s%d" % a, align_bytes=64) for a in range(2)]
+        x_bf = [keep.tile([P, M, 4], BF16, name="x_bf%d" % a, align_bytes=64) for a in range(2)]
+
+        def round_x(a):
+            copy = nc.scalar.copy if a == 0 else nc.vector.tensor_copy
+            copy(
+                x_bf[a][:].rearrange("p (c i) t -> p c t i", i=4),
+                x_raw[a][:].rearrange("p t (c i) -> p c t i", i=4),
+            )
+
+        def quantise_x(a):
+            nc.vector.quantize_mx(x_w[a][:].bitcast(FP8X4), x_s[a][:], x_bf[a][:].rearrange("p m t -> p (m t)"))
+
+        h_w = {}
+        h_s = {}
+        h_pairs = {}
+        h_bf = {}
+
+        def hidden(side, b):
+            pairs = ring.tile([P, 2, M, 2], BF16, name="pairs")
+            h_pairs[side, b] = pairs
+            for t in range(4):
+                acc = psum.tile([P, M], F32, name="acc", tag="p", bufs=3)
+                for a in range(2):
+                    slot = 4 * b + t
+                    if a == 0:
+                        plane = v_s[:, slot, :]
+                    elif side == "next":
+                        plane = v_s1[:, slot, :]
+                    else:
+                        plane = v_s[4:P, slot, :]
+                    if side == "next":
+                        rhs, rhs_scale = xn_w[:, a, :].bitcast(FP4X4), xn_s[:, a, :]
+                    else:
+                        rhs, rhs_scale = x_w[a][:].bitcast(FP8X4), x_s[a][:]
+                    nc.tensor.matmul_mx(acc[:], v_w[a][:, slot, :].bitcast(FP8X4), plane, rhs, rhs_scale, start=(a == 0), stop=(a == 1))
+                nc.scalar.activation(pairs[:, t // 2, :, t % 2], acc[:], ACT.Relu, scale=gain[:, 4 * b + t : 4 * b + t + 1])
+
+        def join_h(side, b):
+            joined = ring.tile([P, M, 2, 2], BF16, name="joined", align_bytes=64)
+            h_bf[side, b] = joined
+            signs = sign[:, 4 * b : 4 * b + 4].rearrange("p (u e) -> p u e", e=2).unsqueeze(1).to_broadcast([P, M, 2, 2])
+            nc.vector.tensor_tensor(joined[:], h_pairs[side, b][:].rearrange("p u m e -> p m u e"), signs, ALU.mult)
+
+        def quantise_h(side, b):
+            h_w[side, b] = keep.tile([P, M], U32, name="h_w_%s%d" % (side, b), align_bytes=64)
+            h_s[side, b] = keep.tile([P, M], U8, name="h_s_%s%d" % (side, b), align_bytes=64)
+            nc.vector.quantize_mx(h_w[side, b][:].bitcast(FP8X4), h_s[side, b][:], h_bf[side, b][:].rearrange("p m u e -> p (m u e)"))
+
+        wd_picked = {}
+        wd_bf = {}
+        wd_w = {}
+        wd_s = {}
+
+        def pick_wd(i):
+            picked = ring.tile([P, 4, P, 2], BF16, name="picked")
+            wd_picked[i] = picked
+            nc.vector.tensor_copy(picked[:].rearrange("p w (q r) e -> p q w e r", r=8), wd_raw[i][:].indirect(offsets[:]))
+
+        def turn_wd(i):
+            turned_bf = ring.tile([P, 2, P, 4], BF16, name="turned_bf", align_bytes=64)
+            wd_bf[i] = turned_bf
+            words = wd_picked[i][:].rearrange("p w c e -> p w (c e)").bitcast(F32)
+            turned = psum.tile([P, 2, 2, P], F32, name="turned", tag="tr", bufs=2)
+            for b in range(2):
+                for u in range(2):
+                    nc.tensor.transpose(turned[:, b, u, :], words[:, 2 * b + u, :], ident[:])
+            nc.scalar.copy(turned_bf[:].bitcast(F32), turned[:].rearrange("p b u n -> p b n u"))
+
+        def quantise_wd(i):
+            wd_w[i] = keep.tile([P, 2 * P], U32, name="wd_w%d" % i, align_bytes=64)
+            wd_s[i] = keep.tile([P, 2 * P], U8, name="wd_s%d" % i, align_bytes=64)
+            nc.vector.quantize_mx(wd_w[i][:].bitcast(FP8X4), wd_s[i][:], wd_bf[i][:].rearrange("p b n t -> p (b n t)"))
+
+        def down(side, i):
+            y = psum.tile([P, M], F32, name="y", tag="y", bufs=3)
+            for b in range(2):
+                cols_n = slice(P * b, P * (b + 1))
+                nc.tensor.matmul_mx(
+                    y[:], wd_w[i][:, cols_n].bitcast(FP8X4), wd_s[i][:, cols_n],
+                    h_w[side, b][:].bitcast(FP8X4), h_s[side, b][:], start=(b == 0), stop=(b == 1),
+                )
+            return y
+
+        discounted = {}
+
+        def discount(i):
+            discounted[i] = keep.tile([P, M], F32, name="discounted%d" % i)
+            nc.vector.tensor_tensor(discounted[i][:], down("next", i)[:], gam_row[:], ALU.mult)
+
+        def finish(i):
+            result = keep.tile([P, M], F32, name="result%d" % i)
+            nc.vector.tensor_tensor(result[:], discounted[i][:], down("now", i)[:], ALU.subtract)
+            nc.sync.dma_start(out[P * i : P * (i + 1), :], result[:])
+
+        round_x(1)
+        round_x(0)
+        quantise_x(1)
+        quantise_x(0)
+        hidden("next", 0)
+        pick_wd(0)
+        turn_wd(0)
+        join_h("next", 0)
+        quantise_h("next", 0)
+        hidden("next", 1)
+        quantise_wd(0)
+        hidden("now", 0)
+        hidden("now", 1)
+        join_h("next", 1)
+        quantise_h("next", 1)
+        pick_wd(1)
+        turn_wd(1)
+        quantise_wd(1)
+        pick_wd(2)
+        turn_wd(2)
+        join_h("now", 0)
+        quantise_h("now", 0)
+        discount(0)
+        pick_wd(3)
+        turn_wd(3)
+        quantise_wd(2)
+        discount(1)
+        join_h("now", 1)
+        quantise_wd(3)
+        quantise_h("now", 1)
+        discount(2)
+        discount(3)
+        finish(0)
+        finish(1)
+        finish(2)
+        finish(3)

@@ -24,6 +24,7 @@ def tile_list_sparse_td_features_kernel(tc, tab_words, tab_scales, offs, x, xn_w
     nc = tc.nc
     with ExitStack() as ctx:
         keep = ctx.enter_context(tc.tile_pool(name="keep", bufs=1))
+        late = ctx.enter_context(tc.tile_pool(name="late", bufs=1))
         ring = ctx.enter_context(tc.tile_pool(name="ring", bufs=2))
         psum = ctx.enter_context(tc.psum_pool(name="psum", bufs=1))
 
@@ -32,16 +33,15 @@ def tile_list_sparse_td_features_kernel(tc, tab_words, tab_scales, offs, x, xn_w
         tab_w = [keep.tile([P, T], U32, name="tab_w%d" % a, align_bytes=64) for a in range(2)]
         xn_w = keep.tile([P, 2, 2 * M], U8, name="xn_w", align_bytes=64)
         xn_s = keep.tile([P, 2, M], U8, name="xn_s", align_bytes=64)
-        v_s_listed = keep.tile([P, S], U8, name="v_s_listed", align_bytes=64)
+        v_s_listed = late.tile([P, S], U8, name="v_s_listed", align_bytes=64, offset=2 * T * 4 - S // 2)
         v_s = keep.tile([P, 8, P], U8, name="v_s", align_bytes=64)
         v_s1 = keep.tile([P, 8, P], U8, name="v_s1", align_bytes=64)
         v_w = [keep.tile([P, 8, P], U32, name="v_w%d" % a, align_bytes=64) for a in range(2)]
-        x_raw = [keep.tile([P, 4, M], F32, name="x_raw%d" % a) for a in range(2)]
-        wd_raw = [keep.tile([P, T], F32, name="wd_raw%d" % i) for i in range(4)]
+        wd_first = keep.tile([P, T], F32, name="wd_first")
         rows = keep.tile([P, P], F32, name="rows")
         ident = keep.tile([P, P], F32, name="ident")
 
-        nc.vector.memset(tab_s[:].bitcast(I32), 0)
+        nc.gpsimd.memset(tab_s[:].bitcast(I32), 0)
         nc.vector.memset(rows[:], 0.0)
         nc.vector.memset(xn_s[:].rearrange("p a c -> p (a c)").bitcast(I32), 0)
         nc.vector.memset(v_s1[:].rearrange("p t c -> p (t c)").bitcast(I32), 0)
@@ -56,29 +56,27 @@ def tile_list_sparse_td_features_kernel(tc, tab_words, tab_scales, offs, x, xn_w
         nc.scalar.dma_start(rows[0:8, :].rearrange("s (q r) -> s q r", r=8), g.rearrange("(q s r) -> s q r", s=8, r=8))
         nc.scalar.dma_start(rows[8:12, :], gam.rearrange("(c p) -> c p", p=P))
         for q in range(4):
-            nc.gpsimd.dma_start(xn_s[32 * q : 32 * q + 4, :, :].bitcast(I32), xn_scales[:, 4 * q : 4 * q + 4, :].rearrange("a r c -> r a c").bitcast(I32))
+            nc.sync.dma_start(xn_s[32 * q : 32 * q + 4, :, :].bitcast(I32), xn_scales[:, 4 * q : 4 * q + 4, :].rearrange("a r c -> r a c").bitcast(I32))
 
-        def load_wd(i):
-            nc.sync.dma_start(wd_raw[i][:], wdT[P * i : P * (i + 1), :])
-
-        def load_x(a):
-            nc.sync.dma_start(x_raw[a][:], x[512 * a : 512 * (a + 1), :].rearrange("(p j) m -> p j m", j=4))
-
-        load_wd(0)
-        load_x(1)
-        load_x(0)
-        for i in range(1, 4):
-            load_wd(i)
+        nc.sync.dma_start(wd_first[:], wdT[0:P, :])
 
         nc.vector.tensor_copy(v_s_listed[:], tab_s[:].indirect(offsets[:]))
         nc.vector.tensor_copy(
             v_s[:].bitcast(I32).rearrange("p s (q w) -> p s q w", w=2),
             v_s_listed[:].bitcast(I32).rearrange("p (q s w) -> p s q w", s=8, w=2),
         )
-        nc.gpsimd.dma_start(
+        nc.sync.dma_start(
             v_s1[0:112, :, :].rearrange("p t c -> p (t c)").bitcast(I32),
             v_s[4:116, :, :].rearrange("p t c -> p (t c)").bitcast(I32),
         )
+        x_late = late.tile([P, 2, 4, M], F32, name="x_late", offset=0)
+        wd_late = late.tile([P, 3, T], F32, name="wd_late", offset=2 * T * 4)
+        x_raw = [x_late[:, a, :, :] for a in range(2)]
+        wd_raw = [wd_first[:]] + [wd_late[:, i, :] for i in range(3)]
+        for a in (1, 0):
+            nc.sync.dma_start(x_raw[a], x[512 * a : 512 * (a + 1), :].rearrange("(p j) m -> p j m", j=4))
+        for i in range(1, 4):
+            nc.sync.dma_start(wd_raw[i], wdT[P * i : P * (i + 1), :])
         for a in range(2):
             nc.vector.tensor_copy(v_w[a][:].rearrange("p s (q r) -> p q s r", r=8), tab_w[a][:].indirect(offsets[:]))
 
@@ -106,7 +104,7 @@ def tile_list_sparse_td_features_kernel(tc, tab_words, tab_scales, offs, x, xn_w
             copy = nc.scalar.copy if a == 0 else nc.vector.tensor_copy
             copy(
                 x_bf[a][:].rearrange("p (c i) t -> p c t i", i=4),
-                x_raw[a][:].rearrange("p t (c i) -> p c t i", i=4),
+                x_raw[a].rearrange("p t (c i) -> p c t i", i=4),
             )
 
         def quantise_x(a):
@@ -156,7 +154,7 @@ def tile_list_sparse_td_features_kernel(tc, tab_words, tab_scales, offs, x, xn_w
         def pick_wd(i):
             picked = ring.tile([P, 4, P, 2], BF16, name="picked")
             wd_picked[i] = picked
-            nc.vector.tensor_copy(picked[:].rearrange("p w (q r) e -> p q w e r", r=8), wd_raw[i][:].indirect(offsets[:]))
+            nc.vector.tensor_copy(picked[:].rearrange("p w (q r) e -> p q w e r", r=8), wd_raw[i].indirect(offsets[:]))
 
         def turn_wd(i):
             turned_bf = ring.tile([P, 2, P, 4], BF16, name="turned_bf", align_bytes=64)

@@ -18,6 +18,9 @@ ALU = mybir.AluOpType
 ACT = mybir.ActivationFunctionType
 
 P = 128
+HIDDEN_BANKS = {"next": (0, 1, 2, 3, 4, 5, 6, 7), "now": (2, 3, 0, 1, 5, 6, 7, 2)}
+TURN_BANKS = (0, 1, 4, 3)
+DOWN_BANKS = {"next": (0, 1, 4, 5), "now": (6, 7, 2, 3)}
 
 
 def tile_list_sparse_td_features_kernel(tc, tab_words, tab_scales, offs, x, xn_words, xn_scales, g, wdT, gam, out):
@@ -25,19 +28,19 @@ def tile_list_sparse_td_features_kernel(tc, tab_words, tab_scales, offs, x, xn_w
     with ExitStack() as ctx:
         keep = ctx.enter_context(tc.tile_pool(name="keep", bufs=1))
         late = ctx.enter_context(tc.tile_pool(name="late", bufs=1))
-        ring = ctx.enter_context(tc.tile_pool(name="ring", bufs=2))
+        ring = ctx.enter_context(tc.tile_pool(name="ring", bufs=3))
         psum = ctx.enter_context(tc.psum_pool(name="psum", bufs=1))
 
         offsets = keep.tile([P, S // 16], U16, name="offsets")
         tab_s = keep.tile([P, T], U8, name="tab_s", align_bytes=64)
-        tab_w = [keep.tile([P, T], U32, name="tab_w%d" % a, align_bytes=64) for a in range(2)]
+        tab_w = [keep.tile([P, T], U32, name="tab_w%d" % a, tag="table%d" % a, align_bytes=64) for a in range(2)]
         xn_w = keep.tile([P, 2, 2 * M], U8, name="xn_w", align_bytes=64)
         xn_s = keep.tile([P, 2, M], U8, name="xn_s", align_bytes=64)
-        v_s_listed = late.tile([P, S], U8, name="v_s_listed", align_bytes=64, offset=2 * T * 4 - S // 2)
+        v_s_listed = late.tile([P, S], U8, name="v_s_listed", align_bytes=64, offset=T * 4 - S // 2)
         v_s = keep.tile([P, 8, P], U8, name="v_s", align_bytes=64)
         v_s1 = keep.tile([P, 8, P], U8, name="v_s1", align_bytes=64)
         v_w = [keep.tile([P, 8, P], U32, name="v_w%d" % a, align_bytes=64) for a in range(2)]
-        wd_first = keep.tile([P, T], F32, name="wd_first")
+        wd_first = keep.tile([P, T], F32, name="wd_first", tag="reused", align_bytes=64)
         rows = keep.tile([P, P], F32, name="rows")
         ident = keep.tile([P, P], F32, name="ident")
 
@@ -45,16 +48,18 @@ def tile_list_sparse_td_features_kernel(tc, tab_words, tab_scales, offs, x, xn_w
         nc.vector.memset(rows[:], 0.0)
         nc.vector.memset(xn_s[:].rearrange("p a c -> p (a c)").bitcast(I32), 0)
         nc.vector.memset(v_s1[:].rearrange("p t c -> p (t c)").bitcast(I32), 0)
+
         make_identity(nc, ident[:])
 
         nc.sync.dma_start(offsets[:], offs)
+        gam_cols = keep.tile([P, 4], F32, name="gam_cols")
+        nc.sync.dma_start(gam_cols[:], gam.rearrange("(p c) -> p c", c=4))
         for q in range(4):
             nc.sync.dma_start(tab_s[32 * q : 32 * q + 8, :].bitcast(I32), tab_scales[:, 4 * q : 4 * q + 4, :].bitcast(I32))
         for a in range(2):
             nc.sync.dma_start(tab_w[a][:].bitcast(I32), tab_words[a].rearrange("p t i -> p (t i)").bitcast(I32))
         nc.sync.dma_start(xn_w[:].bitcast(I32), xn_words.rearrange("a p c -> p a c").bitcast(I32))
-        nc.scalar.dma_start(rows[0:8, :].rearrange("s (q r) -> s q r", r=8), g.rearrange("(q s r) -> s q r", s=8, r=8))
-        nc.scalar.dma_start(rows[8:12, :], gam.rearrange("(c p) -> c p", p=P))
+        nc.gpsimd.dma_start(rows[0:8, :].rearrange("s (q r) -> s q r", r=8), g.rearrange("(q s r) -> s q r", s=8, r=8))
         for q in range(4):
             nc.sync.dma_start(xn_s[32 * q : 32 * q + 4, :, :].bitcast(I32), xn_scales[:, 4 * q : 4 * q + 4, :].rearrange("a r c -> r a c").bitcast(I32))
 
@@ -69,59 +74,62 @@ def tile_list_sparse_td_features_kernel(tc, tab_words, tab_scales, offs, x, xn_w
             v_s1[0:112, :, :].rearrange("p t c -> p (t c)").bitcast(I32),
             v_s[4:116, :, :].rearrange("p t c -> p (t c)").bitcast(I32),
         )
-        x_late = late.tile([P, 2, 4, M], F32, name="x_late", offset=0)
-        wd_late = late.tile([P, 3, T], F32, name="wd_late", offset=2 * T * 4)
-        x_raw = [x_late[:, a, :, :] for a in range(2)]
-        wd_raw = [wd_first[:]] + [wd_late[:, i, :] for i in range(3)]
-        for a in (1, 0):
-            nc.sync.dma_start(x_raw[a], x[512 * a : 512 * (a + 1), :].rearrange("(p j) m -> p j m", j=4))
-        for i in range(1, 4):
-            nc.sync.dma_start(wd_raw[i], wdT[P * i : P * (i + 1), :])
-        for a in range(2):
-            nc.vector.tensor_copy(v_w[a][:].rearrange("p s (q r) -> p q s r", r=8), tab_w[a][:].indirect(offsets[:]))
+        wd_second = late.tile([P, T], F32, name="wd_second", offset=0)
+        nc.sync.dma_start(wd_second[:], wdT[P : 2 * P, :])
+        x_high = late.tile([P, 4, M], F32, name="x_high", offset=T * 4)
+        nc.sync.dma_start(x_high[:], x[512:1024, :].rearrange("(p j) m -> p j m", j=4))
+        nc.vector.tensor_copy(v_w[0][:].rearrange("p s (q r) -> p q s r", r=8), tab_w[0][:].indirect(offsets[:]))
+        x_low = keep.tile([P, 4, M], F32, name="x_low", tag="table0", align_bytes=64)
+        nc.sync.dma_start(x_low[:], x[0:512, :].rearrange("(p j) m -> p j m", j=4))
+        nc.vector.tensor_copy(v_w[1][:].rearrange("p s (q r) -> p q s r", r=8), tab_w[1][:].indirect(offsets[:]))
+        wd_third = keep.tile([P, T], F32, name="wd_third", tag="table1", align_bytes=64)
+        nc.sync.dma_start(wd_third[:], wdT[2 * P : 3 * P, :])
+        x_raw = [x_low[:], x_high[:]]
+        wd_raw = [wd_first[:], wd_second[:], wd_third[:]]
 
-        cols_ps = psum.tile([P, P], F32, name="cols_ps", tag="tr", bufs=2)
+        cols_ps = psum.tile([P, P], F32, name="cols_ps", tag="bank0")
         nc.tensor.transpose(cols_ps[:], rows[:], ident[:])
         gain = keep.tile([P, 8], F32, name="gain")
         sign0 = keep.tile([P, 8], F32, name="sign0")
         sign = keep.tile([P, 8], BF16, name="sign")
-        gam_cols = keep.tile([P, 4], F32, name="gam_cols")
         nc.scalar.activation(gain[:], cols_ps[:, 0:8], ACT.Abs)
         nc.scalar.activation(sign0[:], cols_ps[:, 0:8], ACT.Sign)
-        nc.scalar.copy(gam_cols[:], cols_ps[:, 8:12])
         nc.scalar.activation(sign[:], sign0[:], ACT.Sign, bias=0.5)
         gam_row = keep.tile([P, M], F32, name="gam_row")
-        spread = psum.tile([P, 4, P], F32, name="spread", tag="y", bufs=3)
+        spread = psum.tile([P, 4, P], F32, name="spread", tag="bank7")
         for c in range(4):
             nc.tensor.transpose(spread[:, c, :], gam_cols[:, c : c + 1].to_broadcast([P, P]), ident[:])
-        nc.scalar.copy(gam_row[:], spread[:].rearrange("p c m -> p (c m)"))
+        nc.scalar.copy(gam_row[:].rearrange("p (r c) -> p r c", c=4), spread[:].rearrange("p c r -> p r c"))
 
-        x_w = [keep.tile([P, M], U32, name="x_w%d" % a, align_bytes=64) for a in range(2)]
-        x_s = [keep.tile([P, M], U8, name="x_s%d" % a, align_bytes=64) for a in range(2)]
-        x_bf = [keep.tile([P, M, 4], BF16, name="x_bf%d" % a, align_bytes=64) for a in range(2)]
+        x_w = keep.tile([P, 2, M], U32, name="x_w", align_bytes=64)
+        x_bf = keep.tile([P, 2, M, 4], BF16, name="x_bf", align_bytes=64)
+        x_s = keep.tile([P, 2, M], U8, name="x_s", align_bytes=64)
 
-        def round_x(a):
-            copy = nc.scalar.copy if a == 0 else nc.vector.tensor_copy
-            copy(
-                x_bf[a][:].rearrange("p (c i) t -> p c t i", i=4),
-                x_raw[a].rearrange("p t (c i) -> p c t i", i=4),
+        def quantise(words, scales, rounded):
+            nc.vector.quantize_mx(
+                words.rearrange("p a c -> p (a c)").bitcast(FP8X4),
+                scales.rearrange("p a c -> p (a c)"),
+                rounded.rearrange("p a c t -> p (a c t)"),
             )
 
-        def quantise_x(a):
-            nc.vector.quantize_mx(x_w[a][:].bitcast(FP8X4), x_s[a][:], x_bf[a][:].rearrange("p m t -> p (m t)"))
+        def round_x(copy, a, cols):
+            copy(
+                x_bf[:, a, cols, :].rearrange("p (c i) t -> p c t i", i=4),
+                x_raw[a][:, :, cols].rearrange("p t (c i) -> p c t i", i=4),
+            )
 
-        h_w = {}
-        h_s = {}
+        h_w = {side: keep.tile([P, 2, M], U32, name="h_w_" + side, align_bytes=64) for side in ("next", "now")}
+        h_s = {side: keep.tile([P, 2, M], U8, name="h_s_" + side, align_bytes=64) for side in ("next", "now")}
+        h_bf = {side: keep.tile([P, 2, M, 4], BF16, name="h_bf_" + side, align_bytes=64) for side in ("next", "now")}
         h_pairs = {}
-        h_bf = {}
+
+        sums = {}
 
         def hidden(side, b):
-            pairs = ring.tile([P, 2, M, 2], BF16, name="pairs")
-            h_pairs[side, b] = pairs
             for t in range(4):
-                acc = psum.tile([P, M], F32, name="acc", tag="p", bufs=3)
+                slot = 4 * b + t
+                acc = psum.tile([P, M], F32, name="acc", tag="bank%d" % HIDDEN_BANKS[side][slot])
                 for a in range(2):
-                    slot = 4 * b + t
                     if a == 0:
                         plane = v_s[:, slot, :]
                     elif side == "next":
@@ -131,97 +139,115 @@ def tile_list_sparse_td_features_kernel(tc, tab_words, tab_scales, offs, x, xn_w
                     if side == "next":
                         rhs, rhs_scale = xn_w[:, a, :].bitcast(FP4X4), xn_s[:, a, :]
                     else:
-                        rhs, rhs_scale = x_w[a][:].bitcast(FP8X4), x_s[a][:]
+                        rhs, rhs_scale = x_w[:, a, :].bitcast(FP8X4), x_s[:, a, :]
                     nc.tensor.matmul_mx(acc[:], v_w[a][:, slot, :].bitcast(FP8X4), plane, rhs, rhs_scale, start=(a == 0), stop=(a == 1))
-                nc.scalar.activation(pairs[:, t // 2, :, t % 2], acc[:], ACT.Relu, scale=gain[:, 4 * b + t : 4 * b + t + 1])
+                sums[side, slot] = acc
+
+        def rectify(side, b):
+            if (side, b) == ("next", 1):
+                h_pairs[side, b] = keep.tile([P, 2, M, 2], BF16, name="pairs_after_x", tag="table0", align_bytes=64)
+            else:
+                h_pairs[side, b] = ring.tile([P, 2, M, 2], BF16, name="pairs")
+            for t in range(4):
+                slot = 4 * b + t
+                nc.scalar.activation(h_pairs[side, b][:, t // 2, :, t % 2], sums[side, slot][:], ACT.Relu, scale=gain[:, slot : slot + 1])
 
         def join_h(side, b):
-            joined = ring.tile([P, M, 2, 2], BF16, name="joined", align_bytes=64)
-            h_bf[side, b] = joined
-            signs = sign[:, 4 * b : 4 * b + 4].rearrange("p (u e) -> p u e", e=2).unsqueeze(1).to_broadcast([P, M, 2, 2])
-            nc.vector.tensor_tensor(joined[:], h_pairs[side, b][:].rearrange("p u m e -> p m u e"), signs, ALU.mult)
+            nc.vector.tensor_copy(
+                h_bf[side][:, b, :, :].rearrange("p m (u e) -> p m u e", e=2),
+                h_pairs[side, b][:].rearrange("p u m e -> p m u e"),
+            )
 
-        def quantise_h(side, b):
-            h_w[side, b] = keep.tile([P, M], U32, name="h_w_%s%d" % (side, b), align_bytes=64)
-            h_s[side, b] = keep.tile([P, M], U8, name="h_s_%s%d" % (side, b), align_bytes=64)
-            nc.vector.quantize_mx(h_w[side, b][:].bitcast(FP8X4), h_s[side, b][:], h_bf[side, b][:].rearrange("p m u e -> p (m u e)"))
+        def quantise_h(side, passes):
+            quantise(h_w[side][:, passes, :], h_s[side][:, passes, :], h_bf[side][:, passes, :, :])
 
         wd_picked = {}
-        wd_bf = {}
-        wd_w = {}
-        wd_s = {}
+        wd_turned = {}
+        wd_bf = keep.tile([P, 4, 2 * P, 4], BF16, name="wd_bf", align_bytes=64)
+        wd_w = keep.tile([P, 4, 2 * P], U32, name="wd_w", align_bytes=64)
+        wd_s = keep.tile([P, 4, 2 * P], U8, name="wd_s", align_bytes=64)
 
         def pick_wd(i):
-            picked = ring.tile([P, 4, P, 2], BF16, name="picked")
+            picked = keep.tile([P, 4, P, 2], BF16, name="picked%d" % i)
             wd_picked[i] = picked
             nc.vector.tensor_copy(picked[:].rearrange("p w (q r) e -> p q w e r", r=8), wd_raw[i].indirect(offsets[:]))
 
         def turn_wd(i):
-            turned_bf = ring.tile([P, 2, P, 4], BF16, name="turned_bf", align_bytes=64)
-            wd_bf[i] = turned_bf
             words = wd_picked[i][:].rearrange("p w c e -> p w (c e)").bitcast(F32)
-            turned = psum.tile([P, 2, 2, P], F32, name="turned", tag="tr", bufs=2)
+            turned = psum.tile([P, 2, 2, P], F32, name="turned", tag="bank%d" % TURN_BANKS[i])
+            wd_turned[i] = turned
             for b in range(2):
                 for u in range(2):
-                    nc.tensor.transpose(turned[:, b, u, :], words[:, 2 * b + u, :], ident[:])
-            nc.scalar.copy(turned_bf[:].bitcast(F32), turned[:].rearrange("p b u n -> p b n u"))
+                    nc.tensor.transpose(turned[:, u, b, :], words[:, 2 * b + u, :], ident[:])
 
-        def quantise_wd(i):
-            wd_w[i] = keep.tile([P, 2 * P], U32, name="wd_w%d" % i, align_bytes=64)
-            wd_s[i] = keep.tile([P, 2 * P], U8, name="wd_s%d" % i, align_bytes=64)
-            nc.vector.quantize_mx(wd_w[i][:].bitcast(FP8X4), wd_s[i][:], wd_bf[i][:].rearrange("p b n t -> p (b n t)"))
+        def sign_wd(i):
+            nc.vector.tensor_tensor(
+                wd_bf[:, i, :, :].rearrange("p (b n) (u e) -> p b n u e", b=2, e=2),
+                wd_turned[i][:].bitcast(BF16).rearrange("p u b (n e) -> p b n u e", e=2),
+                sign[:].rearrange("p (b u e) -> p b u e", b=2, e=2).unsqueeze(2).to_broadcast([P, 2, P, 2, 2]),
+                ALU.mult,
+            )
+
+        def quantise_wd(tiles):
+            quantise(wd_w[:, tiles, :], wd_s[:, tiles, :], wd_bf[:, tiles, :, :])
 
         def down(side, i):
-            y = psum.tile([P, M], F32, name="y", tag="y", bufs=3)
+            y = psum.tile([P, M], F32, name="y", tag="bank%d" % DOWN_BANKS[side][i])
             for b in range(2):
                 cols_n = slice(P * b, P * (b + 1))
                 nc.tensor.matmul_mx(
-                    y[:], wd_w[i][:, cols_n].bitcast(FP8X4), wd_s[i][:, cols_n],
-                    h_w[side, b][:].bitcast(FP8X4), h_s[side, b][:], start=(b == 0), stop=(b == 1),
+                    y[:], wd_w[:, i, cols_n].bitcast(FP8X4), wd_s[:, i, cols_n],
+                    h_w[side][:, b, :].bitcast(FP8X4), h_s[side][:, b, :], start=(b == 0), stop=(b == 1),
                 )
             return y
 
-        discounted = {}
+        discounted = keep.tile([P, 4, M], F32, name="discounted")
+        result = keep.tile([P, 4, M], F32, name="result")
 
         def discount(i):
-            discounted[i] = keep.tile([P, M], F32, name="discounted%d" % i)
-            nc.vector.tensor_tensor(discounted[i][:], down("next", i)[:], gam_row[:], ALU.mult)
+            nc.vector.tensor_tensor(discounted[:, i, :], down("next", i)[:], gam_row[:], ALU.mult)
 
         def finish(i):
-            result = keep.tile([P, M], F32, name="result%d" % i)
-            nc.vector.tensor_tensor(result[:], discounted[i][:], down("now", i)[:], ALU.subtract)
-            nc.sync.dma_start(out[P * i : P * (i + 1), :], result[:])
+            nc.vector.tensor_tensor(result[:, i, :], discounted[:, i, :], down("now", i)[:], ALU.subtract)
+            nc.sync.dma_start(out[P * i : P * (i + 1), :], result[:, i, :])
 
-        round_x(1)
-        round_x(0)
-        quantise_x(1)
-        quantise_x(0)
-        hidden("next", 0)
         pick_wd(0)
+        wd_last = keep.tile([P, T], F32, name="wd_last", tag="reused", align_bytes=64)
+        wd_raw.append(wd_last[:])
+        nc.sync.dma_start(wd_last[:], wdT[3 * P : 4 * P, :])
+        hidden("next", 0)
+        rectify("next", 0)
         turn_wd(0)
-        join_h("next", 0)
-        quantise_h("next", 0)
-        hidden("next", 1)
-        quantise_wd(0)
-        hidden("now", 0)
-        hidden("now", 1)
-        join_h("next", 1)
-        quantise_h("next", 1)
         pick_wd(1)
+        round_x(nc.scalar.copy, 0, slice(0, M))
+        sign_wd(0)
+        hidden("next", 1)
         turn_wd(1)
-        quantise_wd(1)
+        join_h("next", 0)
+        round_x(nc.vector.tensor_copy, 1, slice(0, M))
+        sign_wd(1)
+        quantise(x_w[:], x_s[:], x_bf[:])
+        quantise_wd(slice(0, 2))
+        rectify("next", 1)
+        hidden("now", 0)
         pick_wd(2)
         turn_wd(2)
-        join_h("now", 0)
-        quantise_h("now", 0)
-        discount(0)
+        join_h("next", 1)
         pick_wd(3)
+        rectify("now", 0)
+        hidden("now", 1)
+        sign_wd(2)
         turn_wd(3)
-        quantise_wd(2)
-        discount(1)
+        quantise_h("next", slice(0, 2))
+        sign_wd(3)
+        join_h("now", 0)
+        quantise_wd(slice(2, 4))
+        quantise_h("now", slice(0, 1))
+        discount(0)
+        rectify("now", 1)
         join_h("now", 1)
-        quantise_wd(3)
-        quantise_h("now", 1)
+        discount(1)
+        quantise_h("now", slice(1, 2))
         discount(2)
         discount(3)
         finish(0)

@@ -18,239 +18,236 @@ ALU = mybir.AluOpType
 ACT = mybir.ActivationFunctionType
 
 P = 128
-HIDDEN_BANKS = {"next": (0, 1, 2, 3, 4, 5, 6, 7), "now": (2, 3, 0, 1, 5, 6, 7, 2)}
-TURN_BANKS = (0, 1, 4, 3)
-DOWN_BANKS = {"next": (0, 1, 4, 5), "now": (6, 7, 2, 3)}
+RAW = T * 4
+HIDDEN_BANKS = {"next": (0, 1, 2, 3, 4, 5, 6, 7), "now": (1, 2, 3, 0, 4, 5, 6, 7)}
+TURN_BANKS = (0, 1, 2, 3)
+DOWN_BANKS = {"next": (1, 0, 2, 3), "now": (4, 5, 6, 7)}
 
 
 def tile_list_sparse_td_features_kernel(tc, tab_words, tab_scales, offs, x, xn_words, xn_scales, g, wdT, gam, out):
     nc = tc.nc
     with ExitStack() as ctx:
         keep = ctx.enter_context(tc.tile_pool(name="keep", bufs=1))
-        late = ctx.enter_context(tc.tile_pool(name="late", bufs=1))
-        ring = ctx.enter_context(tc.tile_pool(name="ring", bufs=3))
+        arena = ctx.enter_context(tc.tile_pool(name="arena", bufs=1))
+        ring = ctx.enter_context(tc.tile_pool(name="ring", bufs=2))
         psum = ctx.enter_context(tc.psum_pool(name="psum", bufs=1))
 
         offsets = keep.tile([P, S // 16], U16, name="offsets")
         tab_s = keep.tile([P, T], U8, name="tab_s", align_bytes=64)
-        tab_w = [keep.tile([P, T], U32, name="tab_w%d" % a, tag="table%d" % a, align_bytes=64) for a in range(2)]
+        tab_w = [keep.tile([P, T], U32, name="tab_w%d" % a, align_bytes=64) for a in range(2)]
         xn_w = keep.tile([P, 2, 2 * M], U8, name="xn_w", align_bytes=64)
         xn_s = keep.tile([P, 2, M], U8, name="xn_s", align_bytes=64)
-        v_s_listed = late.tile([P, S], U8, name="v_s_listed", align_bytes=64, offset=T * 4 - S // 2)
-        v_s = keep.tile([P, 8, P], U8, name="v_s", align_bytes=64)
-        v_s1 = keep.tile([P, 8, P], U8, name="v_s1", align_bytes=64)
-        v_w = [keep.tile([P, 8, P], U32, name="v_w%d" % a, align_bytes=64) for a in range(2)]
-        wd_first = keep.tile([P, T], F32, name="wd_first", tag="reused", align_bytes=64)
-        rows = keep.tile([P, P], F32, name="rows")
+        v_s_listed = keep.tile([P, S], U8, name="v_s_listed", align_bytes=64)
+        v_s = keep.tile([P, 4, 2 * P], U8, name="v_s", align_bytes=64)
+        v_s1 = keep.tile([P, 4, 2 * P], U8, name="v_s1", align_bytes=64)
+        v_w0 = keep.tile([P, 4, 2 * P], U32, name="v_w0", align_bytes=64)
+        v_w1 = [keep.tile([P, 4, P], U32, name="v_w1_%d" % b, align_bytes=64) for b in range(2)]
+        g_raw = keep.tile([2, 4 * P], F32, name="g_raw")
+        rows = keep.tile([P, 4, P], F32, name="rows")
         ident = keep.tile([P, P], F32, name="ident")
+        wd_raw = [arena.tile([P, T], F32, name="wd_raw%d" % i, align_bytes=64, offset=RAW * i) for i in range(4)]
+        x_raw = [arena.tile([P, 4, M], F32, name="x_raw%d" % a, align_bytes=64, offset=RAW * (4 + a)) for a in range(2)]
+        gam_row = keep.tile([P, M], F32, name="gam_row")
 
         nc.gpsimd.memset(tab_s[:].bitcast(I32), 0)
-        nc.vector.memset(rows[:], 0.0)
         nc.vector.memset(xn_s[:].rearrange("p a c -> p (a c)").bitcast(I32), 0)
         nc.vector.memset(v_s1[:].rearrange("p t c -> p (t c)").bitcast(I32), 0)
-
         make_identity(nc, ident[:])
+        nc.scalar.activation(rows[:], ident[:].unsqueeze(1).to_broadcast([P, 4, P]), ACT.Copy, scale=0.0)
 
         nc.sync.dma_start(offsets[:], offs)
-        gam_cols = keep.tile([P, 4], F32, name="gam_cols")
-        nc.sync.dma_start(gam_cols[:], gam.rearrange("(p c) -> p c", c=4))
+        nc.sync.dma_start(xn_w[:].bitcast(I32), xn_words.rearrange("a p c -> p a c").bitcast(I32))
         for q in range(4):
             nc.sync.dma_start(tab_s[32 * q : 32 * q + 8, :].bitcast(I32), tab_scales[:, 4 * q : 4 * q + 4, :].bitcast(I32))
+        nc.scalar.dma_start(g_raw[:], g.rearrange("(b c) -> b c", b=2))
         for a in range(2):
             nc.sync.dma_start(tab_w[a][:].bitcast(I32), tab_words[a].rearrange("p t i -> p (t i)").bitcast(I32))
-        nc.sync.dma_start(xn_w[:].bitcast(I32), xn_words.rearrange("a p c -> p a c").bitcast(I32))
-        nc.gpsimd.dma_start(rows[0:8, :].rearrange("s (q r) -> s q r", r=8), g.rearrange("(q s r) -> s q r", s=8, r=8))
         for q in range(4):
             nc.sync.dma_start(xn_s[32 * q : 32 * q + 4, :, :].bitcast(I32), xn_scales[:, 4 * q : 4 * q + 4, :].rearrange("a r c -> r a c").bitcast(I32))
 
-        nc.sync.dma_start(wd_first[:], wdT[0:P, :])
-
         nc.vector.tensor_copy(v_s_listed[:], tab_s[:].indirect(offsets[:]))
         nc.vector.tensor_copy(
-            v_s[:].bitcast(I32).rearrange("p s (q w) -> p s q w", w=2),
-            v_s_listed[:].bitcast(I32).rearrange("p (q s w) -> p s q w", s=8, w=2),
+            v_s[:].bitcast(I32).rearrange("p t (c w) -> p t c w", w=2),
+            v_s_listed[:].bitcast(I32).rearrange("p (c t w) -> p t c w", t=4, w=2),
         )
+        nc.sync.dma_start(wd_raw[0][:, 0 : T // 2], wdT[0:P, 0 : T // 2])
         nc.sync.dma_start(
             v_s1[0:112, :, :].rearrange("p t c -> p (t c)").bitcast(I32),
             v_s[4:116, :, :].rearrange("p t c -> p (t c)").bitcast(I32),
         )
-        wd_second = late.tile([P, T], F32, name="wd_second", offset=0)
-        nc.sync.dma_start(wd_second[:], wdT[P : 2 * P, :])
-        x_high = late.tile([P, 4, M], F32, name="x_high", offset=T * 4)
-        nc.sync.dma_start(x_high[:], x[512:1024, :].rearrange("(p j) m -> p j m", j=4))
-        nc.vector.tensor_copy(v_w[0][:].rearrange("p s (q r) -> p q s r", r=8), tab_w[0][:].indirect(offsets[:]))
-        x_low = keep.tile([P, 4, M], F32, name="x_low", tag="table0", align_bytes=64)
-        nc.sync.dma_start(x_low[:], x[0:512, :].rearrange("(p j) m -> p j m", j=4))
-        nc.vector.tensor_copy(v_w[1][:].rearrange("p s (q r) -> p q s r", r=8), tab_w[1][:].indirect(offsets[:]))
-        wd_third = keep.tile([P, T], F32, name="wd_third", tag="table1", align_bytes=64)
-        nc.sync.dma_start(wd_third[:], wdT[2 * P : 3 * P, :])
-        x_raw = [x_low[:], x_high[:]]
-        wd_raw = [wd_first[:], wd_second[:], wd_third[:]]
+        nc.sync.dma_start(wd_raw[0][:, T // 2 : T], wdT[0:P, T // 2 : T])
+        for a in range(2):
+            nc.sync.dma_start(x_raw[a][:], x[512 * a : 512 * (a + 1), :].rearrange("(p j) m -> p j m", j=4))
+        for i in range(1, 4):
+            nc.sync.dma_start(wd_raw[i][:], wdT[P * i : P * (i + 1), :])
+        nc.sync.dma_start(gam_row[:], gam.partition_broadcast(P))
 
-        cols_ps = psum.tile([P, P], F32, name="cols_ps", tag="bank0")
-        nc.tensor.transpose(cols_ps[:], rows[:], ident[:])
-        gain = keep.tile([P, 8], F32, name="gain")
-        sign0 = keep.tile([P, 8], F32, name="sign0")
-        sign = keep.tile([P, 8], BF16, name="sign")
-        nc.scalar.activation(gain[:], cols_ps[:, 0:8], ACT.Abs)
-        nc.scalar.activation(sign0[:], cols_ps[:, 0:8], ACT.Sign)
+        nc.vector.tensor_copy(v_w0[:].rearrange("p t (c r) -> p c t r", r=8), tab_w[0][:].indirect(offsets[:]))
+        for b in range(2):
+            nc.vector.tensor_copy(v_w1[b][:].rearrange("p t (c r) -> p c t r", r=8), tab_w[1][:].indirect(offsets[:, 32 * b : 32 * (b + 1)]))
+
+        nc.scalar.copy(rows[0:2, :, :].rearrange("b t (q r) -> b t q r", r=8), g_raw[:].rearrange("b (q t r) -> b t q r", t=4, r=8))
+        cols_ps = psum.tile([P, 4, P], F32, name="cols_ps", tag="bank7")
+        for t in range(4):
+            nc.tensor.transpose(cols_ps[:, t, :], rows[:, t, :], ident[:])
+        g_cols = cols_ps[:, :, 0:2].rearrange("p t b -> p b t")
+        gain = keep.tile([P, 2, 4], F32, name="gain")
+        sign0 = keep.tile([P, 2, 4], F32, name="sign0")
+        sign = keep.tile([P, 2, 4], BF16, name="sign")
+        nc.scalar.activation(gain[:], g_cols, ACT.Abs)
+        nc.scalar.activation(sign0[:], g_cols, ACT.Sign)
         nc.scalar.activation(sign[:], sign0[:], ACT.Sign, bias=0.5)
-        gam_row = keep.tile([P, M], F32, name="gam_row")
-        spread = psum.tile([P, 4, P], F32, name="spread", tag="bank7")
-        for c in range(4):
-            nc.tensor.transpose(spread[:, c, :], gam_cols[:, c : c + 1].to_broadcast([P, P]), ident[:])
-        nc.scalar.copy(gam_row[:].rearrange("p (r c) -> p r c", c=4), spread[:].rearrange("p c r -> p r c"))
 
-        x_w = keep.tile([P, 2, M], U32, name="x_w", align_bytes=64)
-        x_bf = keep.tile([P, 2, M, 4], BF16, name="x_bf", align_bytes=64)
-        x_s = keep.tile([P, 2, M], U8, name="x_s", align_bytes=64)
+        x_w = [keep.tile([P, M], U32, name="x_w%d" % a, align_bytes=64) for a in range(2)]
+        x_s = [keep.tile([P, M], U8, name="x_s%d" % a, align_bytes=64) for a in range(2)]
+        x_bf = [keep.tile([P, M, 4], BF16, name="x_bf%d" % a, align_bytes=64) for a in range(2)]
 
-        def quantise(words, scales, rounded):
-            nc.vector.quantize_mx(
-                words.rearrange("p a c -> p (a c)").bitcast(FP8X4),
-                scales.rearrange("p a c -> p (a c)"),
-                rounded.rearrange("p a c t -> p (a c t)"),
+        def round_x(a):
+            nc.vector.tensor_copy(
+                x_bf[a][:].rearrange("p (c i) t -> p c t i", i=4),
+                x_raw[a][:].rearrange("p t (c i) -> p c t i", i=4),
             )
 
-        def round_x(copy, a, cols):
-            copy(
-                x_bf[:, a, cols, :].rearrange("p (c i) t -> p c t i", i=4),
-                x_raw[a][:, :, cols].rearrange("p t (c i) -> p c t i", i=4),
-            )
+        def quantise_x(a):
+            nc.vector.quantize_mx(x_w[a][:].bitcast(FP8X4), x_s[a][:], x_bf[a][:].rearrange("p c t -> p (c t)"))
 
-        h_w = {side: keep.tile([P, 2, M], U32, name="h_w_" + side, align_bytes=64) for side in ("next", "now")}
-        h_s = {side: keep.tile([P, 2, M], U8, name="h_s_" + side, align_bytes=64) for side in ("next", "now")}
-        h_bf = {side: keep.tile([P, 2, M, 4], BF16, name="h_bf_" + side, align_bytes=64) for side in ("next", "now")}
-        h_pairs = {}
-
-        sums = {}
+        h_w, h_s, h_bf, h_pairs, sums = {}, {}, {}, {}, {}
 
         def hidden(side, b):
-            for t in range(4):
-                slot = 4 * b + t
-                acc = psum.tile([P, M], F32, name="acc", tag="bank%d" % HIDDEN_BANKS[side][slot])
-                for a in range(2):
+            for t in (0, 2, 1, 3):
+                acc = psum.tile([P, M], F32, name="acc", tag="bank%d" % HIDDEN_BANKS[side][4 * b + t])
+                cols = slice(P * b, P * (b + 1))
+                early = (b == 0 and t % 2 == 0) if side == "next" else b == 0
+                passes = (0, 1) if early else (1, 0)
+                for a in passes:
+                    words = v_w0[:, t, cols] if a == 0 else v_w1[b][:, t, :]
                     if a == 0:
-                        plane = v_s[:, slot, :]
+                        plane = v_s[:, t, cols]
                     elif side == "next":
-                        plane = v_s1[:, slot, :]
+                        plane = v_s1[:, t, cols]
                     else:
-                        plane = v_s[4:P, slot, :]
+                        plane = v_s[4:P, t, cols]
                     if side == "next":
                         rhs, rhs_scale = xn_w[:, a, :].bitcast(FP4X4), xn_s[:, a, :]
                     else:
-                        rhs, rhs_scale = x_w[:, a, :].bitcast(FP8X4), x_s[:, a, :]
-                    nc.tensor.matmul_mx(acc[:], v_w[a][:, slot, :].bitcast(FP8X4), plane, rhs, rhs_scale, start=(a == 0), stop=(a == 1))
-                sums[side, slot] = acc
+                        rhs, rhs_scale = x_w[a][:].bitcast(FP8X4), x_s[a][:]
+                    nc.tensor.matmul_mx(acc[:], words.bitcast(FP8X4), plane, rhs, rhs_scale, start=(a == passes[0]), stop=(a == passes[1]))
+                sums[side, b, t] = acc
 
         def rectify(side, b):
-            if (side, b) == ("next", 1):
-                h_pairs[side, b] = keep.tile([P, 2, M, 2], BF16, name="pairs_after_x", tag="table0", align_bytes=64)
-            else:
-                h_pairs[side, b] = ring.tile([P, 2, M, 2], BF16, name="pairs")
-            for t in range(4):
-                slot = 4 * b + t
-                nc.scalar.activation(h_pairs[side, b][:, t // 2, :, t % 2], sums[side, slot][:], ACT.Relu, scale=gain[:, slot : slot + 1])
+            h_pairs[side, b] = ring.tile([P, 2, M, 2], BF16, name="pairs")
+            for t in (0, 2, 1, 3):
+                nc.scalar.activation(h_pairs[side, b][:, t // 2, :, t % 2], sums[side, b, t][:], ACT.Relu, scale=gain[:, b, t : t + 1])
 
-        def join_h(side, b):
-            nc.vector.tensor_copy(
-                h_bf[side][:, b, :, :].rearrange("p m (u e) -> p m u e", e=2),
-                h_pairs[side, b][:].rearrange("p u m e -> p m u e"),
+        def join_h(copy, side, b):
+            h_bf[side, b] = keep.tile([P, M, 4], BF16, name="h_bf_%s%d" % (side, b), align_bytes=64)
+            copy(
+                h_bf[side, b][:].bitcast(U32),
+                h_pairs[side, b][:].bitcast(U32).rearrange("p u m e -> p m (u e)"),
             )
 
-        def quantise_h(side, passes):
-            quantise(h_w[side][:, passes, :], h_s[side][:, passes, :], h_bf[side][:, passes, :, :])
+        def quantise_h(side, b, place):
+            if place is None:
+                h_w[side, b] = keep.tile([P, M], U32, name="h_w_%s%d" % (side, b), align_bytes=64)
+            else:
+                h_w[side, b] = arena.tile([P, M], U32, name="h_w_%s%d" % (side, b), align_bytes=64, offset=place)
+            h_s[side, b] = keep.tile([P, M], U8, name="h_s_%s%d" % (side, b), align_bytes=64)
+            nc.vector.quantize_mx(h_w[side, b][:].bitcast(FP8X4), h_s[side, b][:], h_bf[side, b][:].rearrange("p c t -> p (c t)"))
 
-        wd_picked = {}
-        wd_turned = {}
-        wd_bf = keep.tile([P, 4, 2 * P, 4], BF16, name="wd_bf", align_bytes=64)
-        wd_w = keep.tile([P, 4, 2 * P], U32, name="wd_w", align_bytes=64)
-        wd_s = keep.tile([P, 4, 2 * P], U8, name="wd_s", align_bytes=64)
+        wd_picked, wd_turned, wd_bf, wd_w, wd_s = {}, {}, {}, {}, {}
 
         def pick_wd(i):
-            picked = keep.tile([P, 4, P, 2], BF16, name="picked%d" % i)
+            picked = keep.tile([P, 2, 2 * P, 2], BF16, name="picked%d" % i)
             wd_picked[i] = picked
-            nc.vector.tensor_copy(picked[:].rearrange("p w (q r) e -> p q w e r", r=8), wd_raw[i].indirect(offsets[:]))
+            nc.vector.tensor_copy(picked[:].rearrange("p u (c r) e -> p c u e r", r=8), wd_raw[i][:].indirect(offsets[:]))
 
         def turn_wd(i):
-            words = wd_picked[i][:].rearrange("p w c e -> p w (c e)").bitcast(F32)
+            words = wd_picked[i][:].rearrange("p u c e -> p u (c e)").bitcast(F32)
             turned = psum.tile([P, 2, 2, P], F32, name="turned", tag="bank%d" % TURN_BANKS[i])
             wd_turned[i] = turned
             for b in range(2):
                 for u in range(2):
-                    nc.tensor.transpose(turned[:, u, b, :], words[:, 2 * b + u, :], ident[:])
+                    nc.tensor.transpose(turned[:, u, b, :], words[:, u, P * b : P * (b + 1)], ident[:])
 
-        def sign_wd(i):
+        def sign_wd(i, place):
+            if place is None:
+                wd_bf[i] = keep.tile([P, 2 * P, 4], BF16, name="wd_bf%d" % i, align_bytes=64)
+            else:
+                wd_bf[i] = arena.tile([P, 2 * P, 4], BF16, name="wd_bf%d" % i, align_bytes=64, offset=place)
             nc.vector.tensor_tensor(
-                wd_bf[:, i, :, :].rearrange("p (b n) (u e) -> p b n u e", b=2, e=2),
+                wd_bf[i][:].rearrange("p (b n) (u e) -> p b n u e", b=2, e=2),
                 wd_turned[i][:].bitcast(BF16).rearrange("p u b (n e) -> p b n u e", e=2),
-                sign[:].rearrange("p (b u e) -> p b u e", b=2, e=2).unsqueeze(2).to_broadcast([P, 2, P, 2, 2]),
+                sign[:].rearrange("p b (u e) -> p b u e", e=2).unsqueeze(2).to_broadcast([P, 2, P, 2, 2]),
                 ALU.mult,
             )
 
-        def quantise_wd(tiles):
-            quantise(wd_w[:, tiles, :], wd_s[:, tiles, :], wd_bf[:, tiles, :, :])
+        def quantise_wd(i, place=None):
+            if place is None:
+                wd_w[i] = keep.tile([P, 2 * P], U32, name="wd_w%d" % i, align_bytes=64)
+            else:
+                wd_w[i] = arena.tile([P, 2 * P], U32, name="wd_w%d" % i, align_bytes=64, offset=place)
+            wd_s[i] = keep.tile([P, 2 * P], U8, name="wd_s%d" % i, align_bytes=64)
+            nc.vector.quantize_mx(wd_w[i][:].bitcast(FP8X4), wd_s[i][:], wd_bf[i][:].rearrange("p c t -> p (c t)"))
 
         def down(side, i):
             y = psum.tile([P, M], F32, name="y", tag="bank%d" % DOWN_BANKS[side][i])
             for b in range(2):
                 cols_n = slice(P * b, P * (b + 1))
                 nc.tensor.matmul_mx(
-                    y[:], wd_w[:, i, cols_n].bitcast(FP8X4), wd_s[:, i, cols_n],
-                    h_w[side][:, b, :].bitcast(FP8X4), h_s[side][:, b, :], start=(b == 0), stop=(b == 1),
+                    y[:], wd_w[i][:, cols_n].bitcast(FP8X4), wd_s[i][:, cols_n],
+                    h_w[side, b][:].bitcast(FP8X4), h_s[side, b][:], start=(b == 0), stop=(b == 1),
                 )
             return y
 
-        discounted = keep.tile([P, 4, M], F32, name="discounted")
-        result = keep.tile([P, 4, M], F32, name="result")
+        discounted = {}
 
-        def discount(i):
-            nc.vector.tensor_tensor(discounted[:, i, :], down("next", i)[:], gam_row[:], ALU.mult)
+        def discount(i, place):
+            discounted[i] = arena.tile([P, M], F32, name="discounted%d" % i, align_bytes=64, offset=place)
+            nc.vector.tensor_tensor(discounted[i][:], down("next", i)[:], gam_row[:], ALU.mult)
 
         def finish(i):
-            nc.vector.tensor_tensor(result[:, i, :], discounted[:, i, :], down("now", i)[:], ALU.subtract)
-            nc.sync.dma_start(out[P * i : P * (i + 1), :], result[:, i, :])
+            result = keep.tile([P, M], F32, name="result%d" % i)
+            nc.vector.tensor_tensor(result[:], discounted[i][:], down("now", i)[:], ALU.subtract)
+            nc.sync.dma_start(out[P * i : P * (i + 1), :], result[:])
 
-        pick_wd(0)
-        wd_last = keep.tile([P, T], F32, name="wd_last", tag="reused", align_bytes=64)
-        wd_raw.append(wd_last[:])
-        nc.sync.dma_start(wd_last[:], wdT[3 * P : 4 * P, :])
         hidden("next", 0)
         rectify("next", 0)
+        pick_wd(0)
         turn_wd(0)
-        pick_wd(1)
-        round_x(nc.scalar.copy, 0, slice(0, M))
-        sign_wd(0)
         hidden("next", 1)
-        turn_wd(1)
-        join_h("next", 0)
-        round_x(nc.vector.tensor_copy, 1, slice(0, M))
-        sign_wd(1)
-        quantise(x_w[:], x_s[:], x_bf[:])
-        quantise_wd(slice(0, 2))
+        join_h(nc.scalar.copy, "next", 0)
+        round_x(0)
+        sign_wd(0, RAW * 4)
+        quantise_x(0)
+        round_x(1)
+        quantise_wd(0, RAW * 5 + 2048)
+        quantise_x(1)
         rectify("next", 1)
+        join_h(nc.scalar.copy, "next", 1)
         hidden("now", 0)
-        pick_wd(2)
-        turn_wd(2)
-        join_h("next", 1)
-        pick_wd(3)
-        rectify("now", 0)
         hidden("now", 1)
-        sign_wd(2)
+        pick_wd(1)
+        quantise_h("next", 0, RAW * 1)
+        rectify("now", 0)
+        turn_wd(1)
+        join_h(nc.scalar.copy, "now", 0)
+        pick_wd(2)
+        quantise_h("next", 1, RAW * 2 + 2048)
+        turn_wd(2)
+        sign_wd(1, RAW * 2)
+        pick_wd(3)
         turn_wd(3)
-        quantise_h("next", slice(0, 2))
-        sign_wd(3)
-        join_h("now", 0)
-        quantise_wd(slice(2, 4))
-        quantise_h("now", slice(0, 1))
-        discount(0)
+        sign_wd(2, RAW * 3)
+        quantise_wd(1, RAW * 3 + 2048)
         rectify("now", 1)
-        join_h("now", 1)
-        discount(1)
-        quantise_h("now", slice(1, 2))
-        discount(2)
-        discount(3)
-        finish(0)
-        finish(1)
-        finish(2)
-        finish(3)
+        join_h(nc.scalar.copy, "now", 1)
+        quantise_h("now", 0, RAW * 3 + 4096)
+        sign_wd(3, None)
+        quantise_wd(2)
+        discount(0, RAW * 0)
+        quantise_wd(3)
+        quantise_h("now", 1, None)
+        for i in range(1, 4):
+            discount(i, RAW * 0 + 2048 * i)
+        for i in range(4):
+            finish(i)

@@ -19,9 +19,11 @@ ACT = mybir.ActivationFunctionType
 
 P = 128
 RAW = T * 4
+AHEAD = 3 * T // 4
+ROUNDED_H = {("next", 0): RAW * 6, ("next", 1): RAW * 6 + 4096, ("now", 0): RAW * 7, ("now", 1): RAW * 7 + 4096}
 HIDDEN_BANKS = {"next": (0, 1, 2, 3, 4, 5, 6, 7), "now": (1, 2, 3, 0, 4, 5, 6, 7)}
-TURN_BANKS = (0, 1, 2, 3)
-DOWN_BANKS = {"next": (1, 0, 2, 3), "now": (4, 5, 6, 7)}
+TURN_BANKS = (0, 1, 3, 2)
+DOWN_BANKS = {"next": (0, 1, 3, 2), "now": (4, 6, 5, 7)}
 
 
 def tile_list_sparse_td_features_kernel(tc, tab_words, tab_scales, offs, x, xn_words, xn_scales, g, wdT, gam, out):
@@ -48,20 +50,22 @@ def tile_list_sparse_td_features_kernel(tc, tab_words, tab_scales, offs, x, xn_w
         wd_raw = [arena.tile([P, T], F32, name="wd_raw%d" % i, align_bytes=64, offset=RAW * i) for i in range(4)]
         x_raw = [arena.tile([P, 4, M], F32, name="x_raw%d" % a, align_bytes=64, offset=RAW * (4 + a)) for a in range(2)]
         gam_row = keep.tile([P, M], F32, name="gam_row")
+        gam_cols = keep.tile([P, 4], F32, name="gam_cols")
 
         nc.gpsimd.memset(tab_s[:].bitcast(I32), 0)
         nc.vector.memset(xn_s[:].rearrange("p a c -> p (a c)").bitcast(I32), 0)
         nc.vector.memset(v_s1[:].rearrange("p t c -> p (t c)").bitcast(I32), 0)
         make_identity(nc, ident[:])
+        nc.scalar.dma_start(g_raw[:], g.rearrange("(b c) -> b c", b=2))
         nc.scalar.activation(rows[:], ident[:].unsqueeze(1).to_broadcast([P, 4, P]), ACT.Copy, scale=0.0)
 
         nc.sync.dma_start(offsets[:], offs)
         nc.sync.dma_start(xn_w[:].bitcast(I32), xn_words.rearrange("a p c -> p a c").bitcast(I32))
         for q in range(4):
             nc.sync.dma_start(tab_s[32 * q : 32 * q + 8, :].bitcast(I32), tab_scales[:, 4 * q : 4 * q + 4, :].bitcast(I32))
-        nc.scalar.dma_start(g_raw[:], g.rearrange("(b c) -> b c", b=2))
         for a in range(2):
             nc.sync.dma_start(tab_w[a][:].bitcast(I32), tab_words[a].rearrange("p t i -> p (t i)").bitcast(I32))
+        nc.sync.dma_start(gam_cols[:], gam.rearrange("(p c) -> p c", c=4))
         for q in range(4):
             nc.sync.dma_start(xn_s[32 * q : 32 * q + 4, :, :].bitcast(I32), xn_scales[:, 4 * q : 4 * q + 4, :].rearrange("a r c -> r a c").bitcast(I32))
 
@@ -70,17 +74,16 @@ def tile_list_sparse_td_features_kernel(tc, tab_words, tab_scales, offs, x, xn_w
             v_s[:].bitcast(I32).rearrange("p t (c w) -> p t c w", w=2),
             v_s_listed[:].bitcast(I32).rearrange("p (c t w) -> p t c w", t=4, w=2),
         )
-        nc.sync.dma_start(wd_raw[0][:, 0 : T // 2], wdT[0:P, 0 : T // 2])
+        nc.sync.dma_start(wd_raw[0][:, 0:AHEAD], wdT[0:P, 0:AHEAD])
         nc.sync.dma_start(
             v_s1[0:112, :, :].rearrange("p t c -> p (t c)").bitcast(I32),
             v_s[4:116, :, :].rearrange("p t c -> p (t c)").bitcast(I32),
         )
-        nc.sync.dma_start(wd_raw[0][:, T // 2 : T], wdT[0:P, T // 2 : T])
+        nc.sync.dma_start(wd_raw[0][:, AHEAD:T], wdT[0:P, AHEAD:T])
         for a in range(2):
             nc.sync.dma_start(x_raw[a][:], x[512 * a : 512 * (a + 1), :].rearrange("(p j) m -> p j m", j=4))
         for i in range(1, 4):
             nc.sync.dma_start(wd_raw[i][:], wdT[P * i : P * (i + 1), :])
-        nc.sync.dma_start(gam_row[:], gam.partition_broadcast(P))
 
         nc.vector.tensor_copy(v_w0[:].rearrange("p t (c r) -> p c t r", r=8), tab_w[0][:].indirect(offsets[:]))
         for b in range(2):
@@ -98,6 +101,11 @@ def tile_list_sparse_td_features_kernel(tc, tab_words, tab_scales, offs, x, xn_w
         nc.scalar.activation(sign0[:], g_cols, ACT.Sign)
         nc.scalar.activation(sign[:], sign0[:], ACT.Sign, bias=0.5)
 
+        spread = psum.tile([P, 4, P], F32, name="spread", tag="bank7")
+        for c in range(4):
+            nc.tensor.transpose(spread[:, c, :], gam_cols[:, c : c + 1].to_broadcast([P, P]), ident[:])
+        nc.scalar.copy(gam_row[:].rearrange("p (r c) -> p r c", c=4), spread[:].rearrange("p c r -> p r c"))
+
         x_w = [keep.tile([P, M], U32, name="x_w%d" % a, align_bytes=64) for a in range(2)]
         x_s = [keep.tile([P, M], U8, name="x_s%d" % a, align_bytes=64) for a in range(2)]
         x_bf = [keep.tile([P, M, 4], BF16, name="x_bf%d" % a, align_bytes=64) for a in range(2)]
@@ -113,8 +121,8 @@ def tile_list_sparse_td_features_kernel(tc, tab_words, tab_scales, offs, x, xn_w
 
         h_w, h_s, h_bf, h_pairs, sums = {}, {}, {}, {}, {}
 
-        def hidden(side, b):
-            for t in (0, 2, 1, 3):
+        def hidden(side, b, codes=(0, 2, 1, 3)):
+            for t in codes:
                 acc = psum.tile([P, M], F32, name="acc", tag="bank%d" % HIDDEN_BANKS[side][4 * b + t])
                 cols = slice(P * b, P * (b + 1))
                 early = (b == 0 and t % 2 == 0) if side == "next" else b == 0
@@ -140,18 +148,18 @@ def tile_list_sparse_td_features_kernel(tc, tab_words, tab_scales, offs, x, xn_w
                 nc.scalar.activation(h_pairs[side, b][:, t // 2, :, t % 2], sums[side, b, t][:], ACT.Relu, scale=gain[:, b, t : t + 1])
 
         def join_h(copy, side, b):
-            h_bf[side, b] = keep.tile([P, M, 4], BF16, name="h_bf_%s%d" % (side, b), align_bytes=64)
+            h_bf[side, b] = arena.tile([P, M, 4], BF16, name="h_bf_%s%d" % (side, b), align_bytes=64, offset=ROUNDED_H[side, b])
             copy(
                 h_bf[side, b][:].bitcast(U32),
                 h_pairs[side, b][:].bitcast(U32).rearrange("p u m e -> p m (u e)"),
             )
 
         def quantise_h(side, b, place):
+            h_w[side, b] = keep.tile([P, M], U32, name="h_w_%s%d" % (side, b), align_bytes=64)
             if place is None:
-                h_w[side, b] = keep.tile([P, M], U32, name="h_w_%s%d" % (side, b), align_bytes=64)
+                h_s[side, b] = keep.tile([P, M], U8, name="h_s_%s%d" % (side, b), align_bytes=64)
             else:
-                h_w[side, b] = arena.tile([P, M], U32, name="h_w_%s%d" % (side, b), align_bytes=64, offset=place)
-            h_s[side, b] = keep.tile([P, M], U8, name="h_s_%s%d" % (side, b), align_bytes=64)
+                h_s[side, b] = arena.tile([P, M], U8, name="h_s_%s%d" % (side, b), align_bytes=64, offset=place)
             nc.vector.quantize_mx(h_w[side, b][:].bitcast(FP8X4), h_s[side, b][:], h_bf[side, b][:].rearrange("p c t -> p (c t)"))
 
         wd_picked, wd_turned, wd_bf, wd_w, wd_s = {}, {}, {}, {}, {}
@@ -205,16 +213,27 @@ def tile_list_sparse_td_features_kernel(tc, tab_words, tab_scales, offs, x, xn_w
             discounted[i] = arena.tile([P, M], F32, name="discounted%d" % i, align_bytes=64, offset=place)
             nc.vector.tensor_tensor(discounted[i][:], down("next", i)[:], gam_row[:], ALU.mult)
 
-        def finish(i):
-            result = keep.tile([P, M], F32, name="result%d" % i)
-            nc.vector.tensor_tensor(result[:], discounted[i][:], down("now", i)[:], ALU.subtract)
-            nc.sync.dma_start(out[P * i : P * (i + 1), :], result[:])
+        def discount_aside(i, place, after):
+            copied = arena.tile([P, M], F32, name="copied%d" % i, align_bytes=64, offset=place)
+            nc.scalar.copy(copied[:], down("next", i)[:])
+            discounted[i] = arena.tile([P, M], F32, name="discounted%d" % i, align_bytes=64, offset=after)
+            nc.gpsimd.tensor_tensor(discounted[i][:], copied[:], gam_row[:], ALU.mult)
+
+        def finish(i, pieces=1):
+            y = down("now", i)
+            width = M // pieces
+            for piece in range(pieces):
+                cols = slice(width * piece, width * (piece + 1))
+                result = keep.tile([P, width], F32, name="result%d_%d" % (i, piece))
+                nc.vector.tensor_tensor(result[:], discounted[i][:, cols], y[:, cols], ALU.subtract)
+                nc.sync.dma_start(out[P * i : P * (i + 1), cols], result[:])
 
         hidden("next", 0)
         rectify("next", 0)
         pick_wd(0)
+        hidden("next", 1, (0,))
         turn_wd(0)
-        hidden("next", 1)
+        hidden("next", 1, (2, 1, 3))
         join_h(nc.scalar.copy, "next", 0)
         round_x(0)
         sign_wd(0, RAW * 4)
@@ -226,28 +245,27 @@ def tile_list_sparse_td_features_kernel(tc, tab_words, tab_scales, offs, x, xn_w
         join_h(nc.scalar.copy, "next", 1)
         hidden("now", 0)
         hidden("now", 1)
-        pick_wd(1)
-        quantise_h("next", 0, RAW * 1)
         rectify("now", 0)
-        turn_wd(1)
         join_h(nc.scalar.copy, "now", 0)
-        pick_wd(2)
-        quantise_h("next", 1, RAW * 2 + 2048)
-        turn_wd(2)
-        sign_wd(1, RAW * 2)
-        pick_wd(3)
-        turn_wd(3)
-        sign_wd(2, RAW * 3)
-        quantise_wd(1, RAW * 3 + 2048)
+        for i in range(1, 4):
+            pick_wd(i)
+            turn_wd(i)
         rectify("now", 1)
         join_h(nc.scalar.copy, "now", 1)
-        quantise_h("now", 0, RAW * 3 + 4096)
+        quantise_h("next", 0, RAW * 3)
+        quantise_h("next", 1, RAW * 3 + 512)
+        sign_wd(1, RAW * 3 + 2048)
+        sign_wd(2, RAW * 3 + 4096)
+        quantise_wd(1)
         sign_wd(3, None)
         quantise_wd(2)
-        discount(0, RAW * 0)
+        quantise_h("now", 0, RAW * 3 + 1024)
         quantise_wd(3)
         quantise_h("now", 1, None)
-        for i in range(1, 4):
-            discount(i, RAW * 0 + 2048 * i)
-        for i in range(4):
+        discount_aside(0, 0, ROUNDED_H["now", 1])
+        discount_aside(1, 2048, ROUNDED_H["now", 1] + 2048)
+        discount(2, 4096)
+        discount(3, 6144)
+        for i in (2, 3, 0):
             finish(i)
+        finish(1, 2)

@@ -21,6 +21,7 @@ P = 128
 RAW = T * 4
 AHEAD = 3 * T // 4
 ROUNDED_H = {("next", 0): RAW * 6, ("next", 1): RAW * 6 + 4096, ("now", 0): RAW * 7, ("now", 1): RAW * 7 + 4096}
+ROUNDED_X = (RAW * 8, RAW * 6 + 2048)
 HIDDEN_BANKS = {"next": (0, 1, 2, 3, 4, 5, 6, 7), "now": (1, 2, 3, 0, 4, 5, 6, 7)}
 TURN_BANKS = (0, 1, 3, 2)
 DOWN_BANKS = {"next": (0, 1, 3, 2), "now": (4, 6, 5, 7)}
@@ -48,7 +49,11 @@ def tile_list_sparse_td_features_kernel(tc, tab_words, tab_scales, offs, x, xn_w
         rows = keep.tile([P, 4, P], F32, name="rows")
         ident = keep.tile([P, P], F32, name="ident")
         wd_raw = [arena.tile([P, T], F32, name="wd_raw%d" % i, align_bytes=64, offset=RAW * i) for i in range(4)]
-        x_raw = [arena.tile([P, 4, M], F32, name="x_raw%d" % a, align_bytes=64, offset=RAW * (4 + a)) for a in range(2)]
+        x_raw = {
+            (a, half): arena.tile([P, 4, M // 2], F32, name="x_raw%d_%d" % (a, half), align_bytes=64, offset=RAW * (4 + a) + RAW // 2 * half)
+            for a in range(2)
+            for half in range(2)
+        }
         gam_row = keep.tile([P, M], F32, name="gam_row")
         gam_cols = keep.tile([P, 4], F32, name="gam_cols")
 
@@ -81,7 +86,9 @@ def tile_list_sparse_td_features_kernel(tc, tab_words, tab_scales, offs, x, xn_w
         )
         nc.sync.dma_start(wd_raw[0][:, AHEAD:T], wdT[0:P, AHEAD:T])
         for a in range(2):
-            nc.sync.dma_start(x_raw[a][:], x[512 * a : 512 * (a + 1), :].rearrange("(p j) m -> p j m", j=4))
+            for half in range(2):
+                cols = slice(M // 2 * half, M // 2 * (half + 1))
+                nc.sync.dma_start(x_raw[a, half][:], x[512 * a : 512 * (a + 1), cols].rearrange("(p j) m -> p j m", j=4))
         for i in range(1, 4):
             nc.sync.dma_start(wd_raw[i][:], wdT[P * i : P * (i + 1), :])
 
@@ -108,12 +115,13 @@ def tile_list_sparse_td_features_kernel(tc, tab_words, tab_scales, offs, x, xn_w
 
         x_w = [keep.tile([P, M], U32, name="x_w%d" % a, align_bytes=64) for a in range(2)]
         x_s = [keep.tile([P, M], U8, name="x_s%d" % a, align_bytes=64) for a in range(2)]
-        x_bf = [keep.tile([P, M, 4], BF16, name="x_bf%d" % a, align_bytes=64) for a in range(2)]
+        x_bf = [arena.tile([P, M, 4], BF16, name="x_bf%d" % a, align_bytes=64, offset=ROUNDED_X[a]) for a in range(2)]
 
-        def round_x(a):
-            nc.vector.tensor_copy(
-                x_bf[a][:].rearrange("p (c i) t -> p c t i", i=4),
-                x_raw[a][:].rearrange("p t (c i) -> p c t i", i=4),
+        def round_x(copy, a, half):
+            cols = slice(M // 2 * half, M // 2 * (half + 1))
+            copy(
+                x_bf[a][:, cols, :].rearrange("p (c i) t -> p c t i", i=4),
+                x_raw[a, half][:].rearrange("p t (c i) -> p c t i", i=4),
             )
 
         def quantise_x(a):
@@ -146,6 +154,15 @@ def tile_list_sparse_td_features_kernel(tc, tab_words, tab_scales, offs, x, xn_w
             h_pairs[side, b] = ring.tile([P, 2, M, 2], BF16, name="pairs")
             for t in (0, 2, 1, 3):
                 nc.scalar.activation(h_pairs[side, b][:, t // 2, :, t % 2], sums[side, b, t][:], ACT.Relu, scale=gain[:, b, t : t + 1])
+
+        def rectify_rows(side, b):
+            h_pairs[side, b] = keep.tile([P, 4, M], BF16, name="h_rows_%s%d" % (side, b))
+            for t in (0, 2, 1, 3):
+                nc.scalar.activation(h_pairs[side, b][:, t, :], sums[side, b, t][:], ACT.Relu, scale=gain[:, b, t : t + 1])
+
+        def weave_h(side, b):
+            h_bf[side, b] = arena.tile([P, M, 4], BF16, name="h_bf_%s%d" % (side, b), align_bytes=64, offset=ROUNDED_H[side, b])
+            nc.gpsimd.tensor_scalar(h_bf[side, b][:], h_pairs[side, b][:].rearrange("p t m -> p m t"), 1.0, 0.0, ALU.mult, ALU.add)
 
         def join_h(copy, side, b):
             h_bf[side, b] = arena.tile([P, M, 4], BF16, name="h_bf_%s%d" % (side, b), align_bytes=64, offset=ROUNDED_H[side, b])
@@ -229,20 +246,22 @@ def tile_list_sparse_td_features_kernel(tc, tab_words, tab_scales, offs, x, xn_w
                 nc.sync.dma_start(out[P * i : P * (i + 1), cols], result[:])
 
         hidden("next", 0)
-        rectify("next", 0)
+        rectify_rows("next", 0)
         pick_wd(0)
-        hidden("next", 1, (0,))
+        hidden("next", 1, (0, 2))
         turn_wd(0)
-        hidden("next", 1, (2, 1, 3))
-        join_h(nc.scalar.copy, "next", 0)
-        round_x(0)
-        sign_wd(0, RAW * 4)
+        hidden("next", 1, (1, 3))
+        round_x(nc.scalar.copy, 0, 0)
+        round_x(nc.vector.tensor_copy, 0, 1)
+        sign_wd(0, RAW * 4 + RAW // 2)
         quantise_x(0)
-        round_x(1)
-        quantise_wd(0, RAW * 5 + 2048)
+        quantise_wd(0)
+        round_x(nc.scalar.copy, 1, 0)
+        round_x(nc.vector.tensor_copy, 1, 1)
         quantise_x(1)
-        rectify("next", 1)
-        join_h(nc.scalar.copy, "next", 1)
+        rectify_rows("next", 1)
+        weave_h("next", 0)
+        weave_h("next", 1)
         hidden("now", 0)
         hidden("now", 1)
         rectify("now", 0)

@@ -22,9 +22,9 @@ RAW = T * 4
 AHEAD = 3 * T // 4
 ROUNDED_H = {("next", 0): RAW * 6, ("next", 1): RAW * 6 + 4096, ("now", 0): RAW * 7, ("now", 1): RAW * 7 + 4096}
 ROUNDED_X = (RAW * 8, RAW * 6 + 2048)
-HIDDEN_BANKS = {"next": (0, 1, 2, 3, 4, 5, 6, 7), "now": (1, 2, 3, 0, 4, 5, 6, 7)}
-TURN_BANKS = (0, 1, 3, 2)
-DOWN_BANKS = {"next": (0, 1, 3, 2), "now": (4, 6, 5, 7)}
+HIDDEN_BANKS = {"next": (0, 1, 2, 3, 4, 5, 6, 7), "now": (1, 2, 3, 0, 4, 0, 6, 4)}
+TURN_BANKS = (0, 5, 7, 1)
+DOWN_BANKS = {"next": (3, 5, 7, 1), "now": (2, 6, 0, 4)}
 
 
 def tile_list_sparse_td_features_kernel(tc, tab_words, tab_scales, offs, x, xn_words, xn_scales, g, wdT, gam, out):
@@ -66,7 +66,7 @@ def tile_list_sparse_td_features_kernel(tc, tab_words, tab_scales, offs, x, xn_w
 
         nc.sync.dma_start(offsets[:], offs)
         nc.sync.dma_start(xn_w[:].bitcast(I32), xn_words.rearrange("a p c -> p a c").bitcast(I32))
-        for q in range(4):
+        for q in (0, 2, 1, 3):
             nc.sync.dma_start(tab_s[32 * q : 32 * q + 8, :].bitcast(I32), tab_scales[:, 4 * q : 4 * q + 4, :].bitcast(I32))
         for a in range(2):
             nc.sync.dma_start(tab_w[a][:].bitcast(I32), tab_words[a].rearrange("p t i -> p (t i)").bitcast(I32))
@@ -124,6 +124,10 @@ def tile_list_sparse_td_features_kernel(tc, tab_words, tab_scales, offs, x, xn_w
                 x_raw[a, half][:].rearrange("p t (c i) -> p c t i", i=4),
             )
 
+        def round_x_aside(a, half):
+            cols = slice(M // 2 * half, M // 2 * (half + 1))
+            nc.gpsimd.tensor_scalar(x_bf[a][:, cols, :], x_raw[a, half][:].rearrange("p t c -> p c t"), 1.0, 0.0, ALU.mult, ALU.add)
+
         def quantise_x(a):
             nc.vector.quantize_mx(x_w[a][:].bitcast(FP8X4), x_s[a][:], x_bf[a][:].rearrange("p c t -> p (c t)"))
 
@@ -150,13 +154,14 @@ def tile_list_sparse_td_features_kernel(tc, tab_words, tab_scales, offs, x, xn_w
                     nc.tensor.matmul_mx(acc[:], words.bitcast(FP8X4), plane, rhs, rhs_scale, start=(a == passes[0]), stop=(a == passes[1]))
                 sums[side, b, t] = acc
 
-        def rectify(side, b):
-            h_pairs[side, b] = ring.tile([P, 2, M, 2], BF16, name="pairs")
-            for t in (0, 2, 1, 3):
+        def rectify(side, b, codes=(0, 2, 1, 3)):
+            if (side, b) not in h_pairs:
+                h_pairs[side, b] = ring.tile([P, 2, M, 2], BF16, name="pairs")
+            for t in codes:
                 nc.scalar.activation(h_pairs[side, b][:, t // 2, :, t % 2], sums[side, b, t][:], ACT.Relu, scale=gain[:, b, t : t + 1])
 
-        def rectify_rows(side, b):
-            h_pairs[side, b] = keep.tile([P, 4, M], BF16, name="h_rows_%s%d" % (side, b))
+        def rectify_rows(side, b, place):
+            h_pairs[side, b] = arena.tile([P, 4, M], BF16, name="h_rows_%s%d" % (side, b), align_bytes=64, offset=place)
             for t in (0, 2, 1, 3):
                 nc.scalar.activation(h_pairs[side, b][:, t, :], sums[side, b, t][:], ACT.Relu, scale=gain[:, b, t : t + 1])
 
@@ -246,30 +251,33 @@ def tile_list_sparse_td_features_kernel(tc, tab_words, tab_scales, offs, x, xn_w
                 nc.sync.dma_start(out[P * i : P * (i + 1), cols], result[:])
 
         hidden("next", 0)
-        rectify_rows("next", 0)
+        rectify_rows("next", 0, RAW * 8 + 4096)
         pick_wd(0)
         hidden("next", 1, (0, 2))
         turn_wd(0)
         hidden("next", 1, (1, 3))
-        round_x(nc.scalar.copy, 0, 0)
+        round_x_aside(0, 0)
         round_x(nc.vector.tensor_copy, 0, 1)
         sign_wd(0, RAW * 4 + RAW // 2)
         quantise_x(0)
         quantise_wd(0)
         round_x(nc.scalar.copy, 1, 0)
-        round_x(nc.vector.tensor_copy, 1, 1)
+        round_x(nc.scalar.copy, 1, 1)
         quantise_x(1)
-        rectify_rows("next", 1)
+        rectify_rows("next", 1, RAW * 5 + RAW // 2)
         weave_h("next", 0)
         weave_h("next", 1)
         hidden("now", 0)
-        hidden("now", 1)
+        hidden("now", 1, (0, 2))
         rectify("now", 0)
         join_h(nc.scalar.copy, "now", 0)
+        hidden("now", 1, (1,))
+        rectify("now", 1, (0,))
+        hidden("now", 1, (3,))
         for i in range(1, 4):
             pick_wd(i)
             turn_wd(i)
-        rectify("now", 1)
+        rectify("now", 1, (2, 1, 3))
         join_h(nc.scalar.copy, "now", 1)
         quantise_h("next", 0, RAW * 3)
         quantise_h("next", 1, RAW * 3 + 512)

@@ -49,11 +49,7 @@ def tile_list_sparse_td_features_kernel(tc, tab_words, tab_scales, offs, x, xn_w
         rows = keep.tile([P, 4, P], F32, name="rows")
         ident = keep.tile([P, P], F32, name="ident")
         wd_raw = [arena.tile([P, T], F32, name="wd_raw%d" % i, align_bytes=64, offset=RAW * i) for i in range(4)]
-        x_raw = {
-            (a, half): arena.tile([P, 4, M // 2], F32, name="x_raw%d_%d" % (a, half), align_bytes=64, offset=RAW * (4 + a) + RAW // 2 * half)
-            for a in range(2)
-            for half in range(2)
-        }
+        x_raw = [arena.tile([P, 4, M], F32, name="x_raw%d" % a, align_bytes=64, offset=RAW * (4 + a)) for a in range(2)]
         gam_row = keep.tile([P, M], F32, name="gam_row")
         gam_cols = keep.tile([P, 4], F32, name="gam_cols")
 
@@ -86,9 +82,7 @@ def tile_list_sparse_td_features_kernel(tc, tab_words, tab_scales, offs, x, xn_w
         )
         nc.sync.dma_start(wd_raw[0][:, AHEAD:T], wdT[0:P, AHEAD:T])
         for a in range(2):
-            for half in range(2):
-                cols = slice(M // 2 * half, M // 2 * (half + 1))
-                nc.sync.dma_start(x_raw[a, half][:], x[512 * a : 512 * (a + 1), cols].rearrange("(p j) m -> p j m", j=4))
+            nc.sync.dma_start(x_raw[a][:], x[512 * a : 512 * (a + 1), :].rearrange("(p j) m -> p j m", j=4))
         for i in range(1, 4):
             nc.sync.dma_start(wd_raw[i][:], wdT[P * i : P * (i + 1), :])
 
@@ -121,12 +115,12 @@ def tile_list_sparse_td_features_kernel(tc, tab_words, tab_scales, offs, x, xn_w
             cols = slice(M // 2 * half, M // 2 * (half + 1))
             copy(
                 x_bf[a][:, cols, :].rearrange("p (c i) t -> p c t i", i=4),
-                x_raw[a, half][:].rearrange("p t (c i) -> p c t i", i=4),
+                x_raw[a][:, :, cols].rearrange("p t (c i) -> p c t i", i=4),
             )
 
         def round_x_aside(a, half):
             cols = slice(M // 2 * half, M // 2 * (half + 1))
-            nc.gpsimd.tensor_scalar(x_bf[a][:, cols, :], x_raw[a, half][:].rearrange("p t c -> p c t"), 1.0, 0.0, ALU.mult, ALU.add)
+            nc.gpsimd.tensor_scalar(x_bf[a][:, cols, :], x_raw[a][:, :, cols].rearrange("p t c -> p c t"), 1.0, 0.0, ALU.mult, ALU.add)
 
         def quantise_x(a):
             nc.vector.quantize_mx(x_w[a][:].bitcast(FP8X4), x_s[a][:], x_bf[a][:].rearrange("p c t -> p (c t)"))
@@ -256,13 +250,13 @@ def tile_list_sparse_td_features_kernel(tc, tab_words, tab_scales, offs, x, xn_w
         hidden("next", 1, (0, 2))
         turn_wd(0)
         hidden("next", 1, (1, 3))
-        round_x_aside(0, 0)
+        round_x(nc.scalar.copy, 0, 0)
         round_x(nc.vector.tensor_copy, 0, 1)
-        sign_wd(0, RAW * 4 + RAW // 2)
+        sign_wd(0, None)
         quantise_x(0)
-        quantise_wd(0)
         round_x(nc.scalar.copy, 1, 0)
-        round_x(nc.scalar.copy, 1, 1)
+        round_x(nc.vector.tensor_copy, 1, 1)
+        quantise_wd(0, RAW * 5)
         quantise_x(1)
         rectify_rows("next", 1, RAW * 5 + RAW // 2)
         weave_h("next", 0)

@@ -23,6 +23,8 @@ AHEAD = 3 * T // 4
 ROUNDED_H = {("next", 0): RAW * 6, ("next", 1): RAW * 6 + 4096, ("now", 0): RAW * 7, ("now", 1): RAW * 7 + 4096}
 ROUNDED_X = (RAW * 8, RAW * 6 + 2048)
 HIDDEN_BANKS = {"next": (0, 1, 2, 3, 4, 5, 6, 7), "now": (1, 2, 3, 0, 4, 0, 6, 4)}
+FIRST_BANKS = (0, 2)
+SPLIT = (M // 2, M // 2)
 TURN_BANKS = (0, 5, 7, 1)
 DOWN_BANKS = {"next": (3, 5, 7, 1), "now": (2, 6, 0, 4)}
 
@@ -111,8 +113,8 @@ def tile_list_sparse_td_features_kernel(tc, tab_words, tab_scales, offs, x, xn_w
         x_s = [keep.tile([P, M], U8, name="x_s%d" % a, align_bytes=64) for a in range(2)]
         x_bf = [arena.tile([P, M, 4], BF16, name="x_bf%d" % a, align_bytes=64, offset=ROUNDED_X[a]) for a in range(2)]
 
-        def round_x(copy, a, half):
-            cols = slice(M // 2 * half, M // 2 * (half + 1))
+        def round_x(copy, a, lo, hi):
+            cols = slice(lo, hi)
             copy(
                 x_bf[a][:, cols, :].rearrange("p (c i) t -> p c t i", i=4),
                 x_raw[a][:, :, cols].rearrange("p t (c i) -> p c t i", i=4),
@@ -205,6 +207,28 @@ def tile_list_sparse_td_features_kernel(tc, tab_words, tab_scales, offs, x, xn_w
                 ALU.mult,
             )
 
+        def first_wd_half(b):
+            picked = keep.tile([P, 2, P, 2], BF16, name="first_picked%d" % b)
+            nc.vector.tensor_copy(picked[:].rearrange("p u (c r) e -> p c u e r", r=8), wd_raw[0][:].indirect(offsets[:, 32 * b : 32 * (b + 1)]))
+            return picked
+
+        def turn_first_half(b, picked):
+            words = picked[:].rearrange("p u c e -> p u (c e)").bitcast(F32)
+            turned = psum.tile([P, 2, P], F32, name="first_turned", tag="bank%d" % FIRST_BANKS[b])
+            for u in range(2):
+                nc.tensor.transpose(turned[:, u, :], words[:, u, :], ident[:])
+            return turned
+
+        def sign_first_half(b, turned):
+            if b == 0:
+                wd_bf[0] = keep.tile([P, 2 * P, 4], BF16, name="wd_bf0", align_bytes=64)
+            nc.vector.tensor_tensor(
+                wd_bf[0][:, P * b : P * (b + 1), :].rearrange("p n (u e) -> p n u e", e=2),
+                turned[:].bitcast(BF16).rearrange("p u (n e) -> p n u e", e=2),
+                sign[:, b, :].rearrange("p (u e) -> p u e", e=2).unsqueeze(1).to_broadcast([P, P, 2, 2]),
+                ALU.mult,
+            )
+
         def quantise_wd(i, place=None):
             if place is None:
                 wd_w[i] = keep.tile([P, 2 * P], U32, name="wd_w%d" % i, align_bytes=64)
@@ -215,11 +239,12 @@ def tile_list_sparse_td_features_kernel(tc, tab_words, tab_scales, offs, x, xn_w
 
         def down(side, i):
             y = psum.tile([P, M], F32, name="y", tag="bank%d" % DOWN_BANKS[side][i])
-            for b in range(2):
+            passes = (1, 0) if side == "now" and i != 2 else (0, 1)
+            for b in passes:
                 cols_n = slice(P * b, P * (b + 1))
                 nc.tensor.matmul_mx(
                     y[:], wd_w[i][:, cols_n].bitcast(FP8X4), wd_s[i][:, cols_n],
-                    h_w[side, b][:].bitcast(FP8X4), h_s[side, b][:], start=(b == 0), stop=(b == 1),
+                    h_w[side, b][:].bitcast(FP8X4), h_s[side, b][:], start=(b == passes[0]), stop=(b == passes[1]),
                 )
             return y
 
@@ -246,16 +271,17 @@ def tile_list_sparse_td_features_kernel(tc, tab_words, tab_scales, offs, x, xn_w
 
         hidden("next", 0)
         rectify_rows("next", 0, RAW * 8 + 4096)
-        pick_wd(0)
+        halves = [first_wd_half(b) for b in range(2)]
         hidden("next", 1, (0, 2))
-        turn_wd(0)
+        halves = [turn_first_half(b, halves[b]) for b in range(2)]
         hidden("next", 1, (1, 3))
-        round_x(nc.scalar.copy, 0, 0)
-        round_x(nc.vector.tensor_copy, 0, 1)
-        sign_wd(0, None)
+        round_x(nc.scalar.copy, 0, 0, SPLIT[0])
+        round_x(nc.vector.tensor_copy, 0, SPLIT[0], M)
+        for b in range(2):
+            sign_first_half(b, halves[b])
         quantise_x(0)
-        round_x(nc.scalar.copy, 1, 0)
-        round_x(nc.vector.tensor_copy, 1, 1)
+        round_x(nc.scalar.copy, 1, 0, SPLIT[1])
+        round_x(nc.vector.tensor_copy, 1, SPLIT[1], M)
         quantise_wd(0, RAW * 5)
         quantise_x(1)
         rectify_rows("next", 1, RAW * 5 + RAW // 2)
@@ -280,11 +306,11 @@ def tile_list_sparse_td_features_kernel(tc, tab_words, tab_scales, offs, x, xn_w
         quantise_wd(1)
         sign_wd(3, None)
         quantise_wd(2)
-        quantise_h("now", 0, RAW * 3 + 1024)
         quantise_wd(3)
+        quantise_h("now", 0, ROUNDED_H["next", 1])
         quantise_h("now", 1, None)
-        discount_aside(0, 0, ROUNDED_H["now", 1])
-        discount_aside(1, 2048, ROUNDED_H["now", 1] + 2048)
+        discount_aside(0, 0, ROUNDED_H["now", 0])
+        discount_aside(1, 2048, ROUNDED_H["now", 1])
         discount(2, 4096)
         discount(3, 6144)
         for i in (2, 3, 0):

@@ -22,11 +22,13 @@ RAW = T * 4
 AHEAD = 3 * T // 4
 ROUNDED_H = {("next", 0): RAW * 6, ("next", 1): RAW * 6 + 4096, ("now", 0): RAW * 7, ("now", 1): RAW * 7 + 4096}
 ROUNDED_X = (RAW * 8, RAW * 6 + 2048)
-HIDDEN_BANKS = {"next": (0, 1, 2, 3, 4, 5, 6, 7), "now": (1, 2, 3, 0, 4, 0, 6, 4)}
+HIDDEN_BANKS = {"next": (0, 1, 2, 3, 4, 5, 6, 7), "now": (1, 2, 3, 0, 4, 7, 6, 2)}
+WOVEN = 3 * M // 8
+LAST_PICKED = RAW * 9 + 512
 FIRST_BANKS = (0, 2)
 SPLIT = (M // 2, M // 2)
-TURN_BANKS = (0, 5, 7, 1)
-DOWN_BANKS = {"next": (3, 5, 7, 1), "now": (2, 6, 0, 4)}
+TURN_BANKS = (0, 5, 4, 1)
+DOWN_BANKS = {"next": (3, 5, 4, 1), "now": (0, 6, 7, 2)}
 
 
 def tile_list_sparse_td_features_kernel(tc, tab_words, tab_scales, offs, x, xn_words, xn_scales, g, wdT, gam, out):
@@ -172,6 +174,19 @@ def tile_list_sparse_td_features_kernel(tc, tab_words, tab_scales, offs, x, xn_w
                 h_pairs[side, b][:].bitcast(U32).rearrange("p u m e -> p m (u e)"),
             )
 
+        def rectify_shared(side, b, place):
+            rows_part = arena.tile([P, 4, WOVEN], BF16, name="shared_rows", align_bytes=64, offset=place)
+            pairs_part = keep.tile([P, 2, M - WOVEN, 2], BF16, name="shared_pairs")
+            for t in (0, 2, 1, 3):
+                nc.scalar.activation(rows_part[:, t, :], sums[side, b, t][:, 0:WOVEN], ACT.Relu, scale=gain[:, b, t : t + 1])
+                nc.scalar.activation(pairs_part[:, t // 2, :, t % 2], sums[side, b, t][:, WOVEN:M], ACT.Relu, scale=gain[:, b, t : t + 1])
+            h_bf[side, b] = arena.tile([P, M, 4], BF16, name="h_bf_%s%d" % (side, b), align_bytes=64, offset=ROUNDED_H[side, b])
+            nc.gpsimd.tensor_scalar(h_bf[side, b][:, 0:WOVEN, :], rows_part[:].rearrange("p t m -> p m t"), 1.0, 0.0, ALU.mult, ALU.add)
+            nc.scalar.copy(
+                h_bf[side, b][:, WOVEN:M, :].bitcast(U32),
+                pairs_part[:].bitcast(U32).rearrange("p u m e -> p m (u e)"),
+            )
+
         def quantise_h(side, b, place):
             h_w[side, b] = keep.tile([P, M], U32, name="h_w_%s%d" % (side, b), align_bytes=64)
             if place is None:
@@ -206,6 +221,16 @@ def tile_list_sparse_td_features_kernel(tc, tab_words, tab_scales, offs, x, xn_w
                 sign[:].rearrange("p b (u e) -> p b u e", e=2).unsqueeze(2).to_broadcast([P, 2, P, 2, 2]),
                 ALU.mult,
             )
+
+        def last_wd():
+            turned = psum.tile([P, 2, 2, P], F32, name="turned", tag="bank%d" % TURN_BANKS[3])
+            wd_turned[3] = turned
+            for b in range(2):
+                picked = arena.tile([P, 2, P, 2], BF16, name="last_picked%d" % b, align_bytes=64, offset=LAST_PICKED + 4096 * b)
+                nc.vector.tensor_copy(picked[:].rearrange("p u (c r) e -> p c u e r", r=8), wd_raw[3][:].indirect(offsets[:, 32 * b : 32 * (b + 1)]))
+                words = picked[:].rearrange("p u c e -> p u (c e)").bitcast(F32)
+                for u in range(2):
+                    nc.tensor.transpose(turned[:, u, b, :], words[:, u, :], ident[:])
 
         def first_wd_half(b):
             picked = keep.tile([P, 2, P, 2], BF16, name="first_picked%d" % b)
@@ -289,20 +314,19 @@ def tile_list_sparse_td_features_kernel(tc, tab_words, tab_scales, offs, x, xn_w
         weave_h("next", 1)
         hidden("now", 0)
         hidden("now", 1, (0, 2))
-        rectify("now", 0)
-        join_h(nc.scalar.copy, "now", 0)
-        hidden("now", 1, (1,))
+        rectify_shared("now", 0, RAW * 4)
+        hidden("now", 1, (1, 3))
         rectify("now", 1, (0,))
-        hidden("now", 1, (3,))
-        for i in range(1, 4):
+        for i in (1, 2):
             pick_wd(i)
             turn_wd(i)
+        last_wd()
         rectify("now", 1, (2, 1, 3))
         join_h(nc.scalar.copy, "now", 1)
-        quantise_h("next", 0, RAW * 3)
-        quantise_h("next", 1, RAW * 3 + 512)
-        sign_wd(1, RAW * 3 + 2048)
-        sign_wd(2, RAW * 3 + 4096)
+        quantise_h("next", 0, LAST_PICKED - 448)
+        quantise_h("next", 1, LAST_PICKED + 128)
+        sign_wd(1, LAST_PICKED + 960)
+        sign_wd(2, ROUNDED_H["next", 0])
         quantise_wd(1)
         sign_wd(3, None)
         quantise_wd(2)

@@ -22,13 +22,12 @@ RAW = T * 4
 AHEAD = 3 * T // 4
 ROUNDED_H = {("next", 0): RAW * 6, ("next", 1): RAW * 6 + 4096, ("now", 0): RAW * 7, ("now", 1): RAW * 7 + 4096}
 ROUNDED_X = (RAW * 8, RAW * 6 + 2048)
-HIDDEN_BANKS = {"next": (0, 1, 2, 3, 4, 5, 6, 7), "now": (1, 2, 3, 0, 4, 7, 6, 2)}
-WOVEN = 3 * M // 8
+HIDDEN_BANKS = {"next": (0, 1, 2, 3, 4, 5, 6, 7), "now": (1, 2, 3, 0, 4, 7, 6, 1)}
 LAST_PICKED = RAW * 9 + 512
 FIRST_BANKS = (0, 2)
 SPLIT = (M // 2, M // 2)
-TURN_BANKS = (0, 5, 4, 1)
-DOWN_BANKS = {"next": (3, 5, 4, 1), "now": (0, 6, 7, 2)}
+TURN_BANKS = (0, 5, 3, 2)
+DOWN_BANKS = {"next": (0, 5, 3, 2), "now": (4, 6, 7, 1)}
 
 
 def tile_list_sparse_td_features_kernel(tc, tab_words, tab_scales, offs, x, xn_words, xn_scales, g, wdT, gam, out):
@@ -174,19 +173,6 @@ def tile_list_sparse_td_features_kernel(tc, tab_words, tab_scales, offs, x, xn_w
                 h_pairs[side, b][:].bitcast(U32).rearrange("p u m e -> p m (u e)"),
             )
 
-        def rectify_shared(side, b, place):
-            rows_part = arena.tile([P, 4, WOVEN], BF16, name="shared_rows", align_bytes=64, offset=place)
-            pairs_part = keep.tile([P, 2, M - WOVEN, 2], BF16, name="shared_pairs")
-            for t in (0, 2, 1, 3):
-                nc.scalar.activation(rows_part[:, t, :], sums[side, b, t][:, 0:WOVEN], ACT.Relu, scale=gain[:, b, t : t + 1])
-                nc.scalar.activation(pairs_part[:, t // 2, :, t % 2], sums[side, b, t][:, WOVEN:M], ACT.Relu, scale=gain[:, b, t : t + 1])
-            h_bf[side, b] = arena.tile([P, M, 4], BF16, name="h_bf_%s%d" % (side, b), align_bytes=64, offset=ROUNDED_H[side, b])
-            nc.gpsimd.tensor_scalar(h_bf[side, b][:, 0:WOVEN, :], rows_part[:].rearrange("p t m -> p m t"), 1.0, 0.0, ALU.mult, ALU.add)
-            nc.scalar.copy(
-                h_bf[side, b][:, WOVEN:M, :].bitcast(U32),
-                pairs_part[:].bitcast(U32).rearrange("p u m e -> p m (u e)"),
-            )
-
         def quantise_h(side, b, place):
             h_w[side, b] = keep.tile([P, M], U32, name="h_w_%s%d" % (side, b), align_bytes=64)
             if place is None:
@@ -314,7 +300,8 @@ def tile_list_sparse_td_features_kernel(tc, tab_words, tab_scales, offs, x, xn_w
         weave_h("next", 1)
         hidden("now", 0)
         hidden("now", 1, (0, 2))
-        rectify_shared("now", 0, RAW * 4)
+        rectify("now", 0)
+        join_h(nc.scalar.copy, "now", 0)
         hidden("now", 1, (1, 3))
         rectify("now", 1, (0,))
         for i in (1, 2):

@@ -73,11 +73,14 @@ def tile_list_sparse_td_features_kernel(tc, tab_words, tab_scales, offs, x, xn_w
         for q in range(4):
             nc.sync.dma_start(xn_s[32 * q : 32 * q + 4, :, :].bitcast(I32), xn_scales[:, 4 * q : 4 * q + 4, :].rearrange("a r c -> r a c").bitcast(I32))
 
-        nc.vector.tensor_copy(v_s_listed[:], tab_s[:].indirect(offsets[:]))
-        nc.vector.tensor_copy(
-            v_s[:].bitcast(I32).rearrange("p t (c w) -> p t c w", w=2),
-            v_s_listed[:].bitcast(I32).rearrange("p (c t w) -> p t c w", t=4, w=2),
-        )
+        parts = ((0, 3 * S // 4), (3 * S // 4, S))
+        for lo, hi in parts:
+            nc.vector.tensor_copy(v_s_listed[:, lo:hi], tab_s[:].indirect(offsets[:, lo // 16 : hi // 16]))
+        for lo, hi in parts:
+            nc.vector.tensor_copy(
+                v_s[:, :, lo // 4 : hi // 4].bitcast(I32).rearrange("p t (c w) -> p t c w", w=2),
+                v_s_listed[:, lo:hi].bitcast(I32).rearrange("p (c t w) -> p t c w", t=4, w=2),
+            )
         nc.sync.dma_start(wd_raw[0][:, 0:AHEAD], wdT[0:P, 0:AHEAD])
         nc.sync.dma_start(
             v_s1[0:112, :, :].rearrange("p t c -> p (t c)").bitcast(I32),
@@ -291,10 +294,12 @@ def tile_list_sparse_td_features_kernel(tc, tab_words, tab_scales, offs, x, xn_w
         for b in range(2):
             sign_first_half(b, halves[b])
         quantise_x(0)
-        round_x(nc.scalar.copy, 1, 0, SPLIT[1])
-        round_x(nc.vector.tensor_copy, 1, SPLIT[1], M)
-        quantise_wd(0, RAW * 5)
-        quantise_x(1)
+        quantise_wd(0)
+        round_x(nc.scalar.copy, 1, 0, M // 4)
+        round_x(nc.scalar.copy, 1, M // 4, M // 2)
+        round_x(nc.vector.tensor_copy, 1, M // 2, M)
+        for lo, hi in ((0, M // 4), (M // 2, M), (M // 4, M // 2)):
+            nc.vector.quantize_mx(x_w[1][:, lo:hi].bitcast(FP8X4), x_s[1][:, lo:hi], x_bf[1][:, lo:hi, :].rearrange("p c t -> p (c t)"))
         rectify_rows("next", 1, RAW * 5 + RAW // 2)
         weave_h("next", 0)
         weave_h("next", 1)

@@ -70,8 +70,8 @@ def tile_list_sparse_td_features_kernel(tc, tab_words, tab_scales, offs, x, xn_w
         for a in range(2):
             nc.sync.dma_start(tab_w[a][:].bitcast(I32), tab_words[a].rearrange("p t i -> p (t i)").bitcast(I32))
         nc.sync.dma_start(gam_cols[:], gam.rearrange("(p c) -> p c", c=4))
-        for q in range(4):
-            nc.sync.dma_start(xn_s[32 * q : 32 * q + 4, :, :].bitcast(I32), xn_scales[:, 4 * q : 4 * q + 4, :].rearrange("a r c -> r a c").bitcast(I32))
+        for r in range(4):
+            nc.sync.dma_start(xn_s[r:P:32, :, :].bitcast(I32), xn_scales[:, r:16:4, :].rearrange("a q c -> q a c").bitcast(I32))
 
         parts = ((0, 3 * S // 4), (3 * S // 4, S))
         for lo, hi in parts:

@@ -19,15 +19,17 @@ ACT = mybir.ActivationFunctionType
 
 P = 128
 RAW = T * 4
+KIB = 1024
 AHEAD = 3 * T // 4
-ROUNDED_H = {("next", 0): RAW * 6, ("next", 1): RAW * 6 + 4096, ("now", 0): RAW * 7, ("now", 1): RAW * 7 + 4096}
-ROUNDED_X = (RAW * 8, RAW * 6 + 2048)
-HIDDEN_BANKS = {"next": (0, 1, 2, 3, 4, 5, 6, 7), "now": (1, 2, 3, 0, 4, 7, 6, 1)}
-LAST_PICKED = RAW * 9 + 512
 FIRST_BANKS = (0, 2)
-SPLIT = (M // 2, M // 2)
-TURN_BANKS = (0, 5, 3, 2)
-DOWN_BANKS = {"next": (0, 5, 3, 2), "now": (4, 6, 7, 1)}
+ROUNDED_X = (48 * KIB, 92 * KIB)
+PICKED_HALVES = {1: (RAW * 4, RAW * 4 + 1024), 3: (62 * KIB, 63 * KIB)}
+PAIRS = 68 * KIB
+ROWS = {("next", 0): 104 * KIB, ("next", 1): RAW * 4 + 4096, ("now", 0): 112 * KIB}
+ROUNDED_H = {("next", 0): ROUNDED_X[0], ("next", 1): 104 * KIB - 4096 + 64, ("now", 0): 76 * KIB, ("now", 1): 80 * KIB}
+HIDDEN_BANKS = {"next": (0, 1, 2, 3, 4, 5, 6, 7), "now": (1, 4, 3, 6, 5, 4, 7, 6)}
+TURN_BANKS = (0, 2, 0, 2)
+DOWN_BANKS = {"next": (4, 6, 1, 3), "now": (5, 7, 0, 2)}
 
 
 def tile_list_sparse_td_features_kernel(tc, tab_words, tab_scales, offs, x, xn_words, xn_scales, g, wdT, gam, out):
@@ -35,7 +37,6 @@ def tile_list_sparse_td_features_kernel(tc, tab_words, tab_scales, offs, x, xn_w
     with ExitStack() as ctx:
         keep = ctx.enter_context(tc.tile_pool(name="keep", bufs=1))
         arena = ctx.enter_context(tc.tile_pool(name="arena", bufs=1))
-        ring = ctx.enter_context(tc.tile_pool(name="ring", bufs=2))
         psum = ctx.enter_context(tc.psum_pool(name="psum", bufs=1))
 
         offsets = keep.tile([P, S // 16], U16, name="offsets")
@@ -81,15 +82,17 @@ def tile_list_sparse_td_features_kernel(tc, tab_words, tab_scales, offs, x, xn_w
                 v_s[:, :, lo // 4 : hi // 4].bitcast(I32).rearrange("p t (c w) -> p t c w", w=2),
                 v_s_listed[:, lo:hi].bitcast(I32).rearrange("p (c t w) -> p t c w", t=4, w=2),
             )
+        x_rows = [x[512 * a : 512 * (a + 1), :].rearrange("(p j) m -> p j m", j=4) for a in range(2)]
         nc.sync.dma_start(wd_raw[0][:, 0:AHEAD], wdT[0:P, 0:AHEAD])
         nc.sync.dma_start(
             v_s1[0:112, :, :].rearrange("p t c -> p (t c)").bitcast(I32),
             v_s[4:116, :, :].rearrange("p t c -> p (t c)").bitcast(I32),
         )
         nc.sync.dma_start(wd_raw[0][:, AHEAD:T], wdT[0:P, AHEAD:T])
-        for a in range(2):
-            nc.sync.dma_start(x_raw[a][:], x[512 * a : 512 * (a + 1), :].rearrange("(p j) m -> p j m", j=4))
-        for i in range(1, 4):
+        nc.sync.dma_start(x_raw[0][:], x_rows[0])
+        nc.sync.dma_start(wd_raw[1][:], wdT[P : 2 * P, :])
+        nc.sync.dma_start(x_raw[1][:], x_rows[1])
+        for i in range(2, 4):
             nc.sync.dma_start(wd_raw[i][:], wdT[P * i : P * (i + 1), :])
 
         nc.vector.tensor_copy(v_w0[:].rearrange("p t (c r) -> p c t r", r=8), tab_w[0][:].indirect(offsets[:]))
@@ -137,7 +140,7 @@ def tile_list_sparse_td_features_kernel(tc, tab_words, tab_scales, offs, x, xn_w
             for t in codes:
                 acc = psum.tile([P, M], F32, name="acc", tag="bank%d" % HIDDEN_BANKS[side][4 * b + t])
                 cols = slice(P * b, P * (b + 1))
-                early = (b == 0 and t % 2 == 0) if side == "next" else b == 0
+                early = (b == 0 and t % 2 == 0) if side == "next" else True
                 passes = (0, 1) if early else (1, 0)
                 for a in passes:
                     words = v_w0[:, t, cols] if a == 0 else v_w1[b][:, t, :]
@@ -156,12 +159,12 @@ def tile_list_sparse_td_features_kernel(tc, tab_words, tab_scales, offs, x, xn_w
 
         def rectify(side, b, codes=(0, 2, 1, 3)):
             if (side, b) not in h_pairs:
-                h_pairs[side, b] = ring.tile([P, 2, M, 2], BF16, name="pairs")
+                h_pairs[side, b] = arena.tile([P, 2, M, 2], BF16, name="pairs", align_bytes=64, offset=PAIRS)
             for t in codes:
                 nc.scalar.activation(h_pairs[side, b][:, t // 2, :, t % 2], sums[side, b, t][:], ACT.Relu, scale=gain[:, b, t : t + 1])
 
-        def rectify_rows(side, b, place):
-            h_pairs[side, b] = arena.tile([P, 4, M], BF16, name="h_rows_%s%d" % (side, b), align_bytes=64, offset=place)
+        def rectify_rows(side, b):
+            h_pairs[side, b] = arena.tile([P, 4, M], BF16, name="h_rows_%s%d" % (side, b), align_bytes=64, offset=ROWS[side, b])
             for t in (0, 2, 1, 3):
                 nc.scalar.activation(h_pairs[side, b][:, t, :], sums[side, b, t][:], ACT.Relu, scale=gain[:, b, t : t + 1])
 
@@ -186,8 +189,8 @@ def tile_list_sparse_td_features_kernel(tc, tab_words, tab_scales, offs, x, xn_w
 
         wd_picked, wd_turned, wd_bf, wd_w, wd_s = {}, {}, {}, {}, {}
 
-        def pick_wd(i):
-            picked = keep.tile([P, 2, 2 * P, 2], BF16, name="picked%d" % i)
+        def pick_wd(i, place):
+            picked = arena.tile([P, 2, 2 * P, 2], BF16, name="picked%d" % i, align_bytes=64, offset=place)
             wd_picked[i] = picked
             nc.vector.tensor_copy(picked[:].rearrange("p u (c r) e -> p c u e r", r=8), wd_raw[i][:].indirect(offsets[:]))
 
@@ -211,12 +214,12 @@ def tile_list_sparse_td_features_kernel(tc, tab_words, tab_scales, offs, x, xn_w
                 ALU.mult,
             )
 
-        def last_wd():
-            turned = psum.tile([P, 2, 2, P], F32, name="turned", tag="bank%d" % TURN_BANKS[3])
-            wd_turned[3] = turned
+        def pick_and_turn_halves(i):
+            turned = psum.tile([P, 2, 2, P], F32, name="turned", tag="bank%d" % TURN_BANKS[i])
+            wd_turned[i] = turned
             for b in range(2):
-                picked = arena.tile([P, 2, P, 2], BF16, name="last_picked%d" % b, align_bytes=64, offset=LAST_PICKED + 4096 * b)
-                nc.vector.tensor_copy(picked[:].rearrange("p u (c r) e -> p c u e r", r=8), wd_raw[3][:].indirect(offsets[:, 32 * b : 32 * (b + 1)]))
+                picked = arena.tile([P, 2, P, 2], BF16, name="picked%d_%d" % (i, b), align_bytes=64, offset=PICKED_HALVES[i][b])
+                nc.vector.tensor_copy(picked[:].rearrange("p u (c r) e -> p c u e r", r=8), wd_raw[i][:].indirect(offsets[:, 32 * b : 32 * (b + 1)]))
                 words = picked[:].rearrange("p u c e -> p u (c e)").bitcast(F32)
                 for u in range(2):
                     nc.tensor.transpose(turned[:, u, b, :], words[:, u, :], ident[:])
@@ -251,31 +254,37 @@ def tile_list_sparse_td_features_kernel(tc, tab_words, tab_scales, offs, x, xn_w
             wd_s[i] = keep.tile([P, 2 * P], U8, name="wd_s%d" % i, align_bytes=64)
             nc.vector.quantize_mx(wd_w[i][:].bitcast(FP8X4), wd_s[i][:], wd_bf[i][:].rearrange("p c t -> p (c t)"))
 
-        def down(side, i):
-            y = psum.tile([P, M], F32, name="y", tag="bank%d" % DOWN_BANKS[side][i])
-            passes = (1, 0) if side == "now" and i != 2 else (0, 1)
+        sums_down = {}
+
+        def down(side, i, passes=(0, 1)):
+            if (side, i) not in sums_down:
+                sums_down[side, i] = psum.tile([P, M], F32, name="y", tag="bank%d" % DOWN_BANKS[side][i])
+            y = sums_down[side, i]
+            first = 1 if side == "now" and i < 2 else 0
             for b in passes:
                 cols_n = slice(P * b, P * (b + 1))
                 nc.tensor.matmul_mx(
                     y[:], wd_w[i][:, cols_n].bitcast(FP8X4), wd_s[i][:, cols_n],
-                    h_w[side, b][:].bitcast(FP8X4), h_s[side, b][:], start=(b == passes[0]), stop=(b == passes[1]),
+                    h_w[side, b][:].bitcast(FP8X4), h_s[side, b][:], start=(b == first), stop=(b != first),
                 )
             return y
 
         discounted = {}
+        copied = arena.tile([P, 2, M], F32, name="copied", align_bytes=64, offset=PAIRS - 4096 + 64)
+        discounted_late = arena.tile([P, 2, M], F32, name="discounted_late", align_bytes=64, offset=PAIRS + 4096 - 64)
 
-        def discount(i, place):
-            discounted[i] = arena.tile([P, M], F32, name="discounted%d" % i, align_bytes=64, offset=place)
-            nc.vector.tensor_tensor(discounted[i][:], down("next", i)[:], gam_row[:], ALU.mult)
+        def discount(i):
+            discounted[i] = discounted_late[:, i - 2, :]
+            nc.vector.tensor_tensor(discounted[i], sums_down["next", i][:], gam_row[:], ALU.mult)
 
-        def discount_aside(i, place, after):
-            copied = arena.tile([P, M], F32, name="copied%d" % i, align_bytes=64, offset=place)
-            nc.scalar.copy(copied[:], down("next", i)[:])
-            discounted[i] = arena.tile([P, M], F32, name="discounted%d" % i, align_bytes=64, offset=after)
-            nc.gpsimd.tensor_tensor(discounted[i][:], copied[:], gam_row[:], ALU.mult)
+        def discount_aside(i):
+            nc.scalar.copy(copied[:, i, :], sums_down["next", i][:])
+            aside = arena.tile([P, M], F32, name="discounted%d" % i, align_bytes=64, offset=ROUNDED_H["now", i])
+            discounted[i] = aside[:]
+            nc.gpsimd.tensor_tensor(discounted[i], copied[:, i, :], gam_row[:], ALU.mult)
 
         def finish(i, pieces=1):
-            y = down("now", i)
+            y = sums_down["now", i]
             width = M // pieces
             for piece in range(pieces):
                 cols = slice(width * piece, width * (piece + 1))
@@ -283,52 +292,62 @@ def tile_list_sparse_td_features_kernel(tc, tab_words, tab_scales, offs, x, xn_w
                 nc.vector.tensor_tensor(result[:], discounted[i][:, cols], y[:, cols], ALU.subtract)
                 nc.sync.dma_start(out[P * i : P * (i + 1), cols], result[:])
 
+        round_x(nc.scalar.copy, 0, 0, M // 2)
+        round_x_aside(0, 1)
         hidden("next", 0)
-        rectify_rows("next", 0, RAW * 8 + 4096)
+        rectify_rows("next", 0)
         halves = [first_wd_half(b) for b in range(2)]
         hidden("next", 1, (0, 2))
         halves = [turn_first_half(b, halves[b]) for b in range(2)]
         hidden("next", 1, (1, 3))
-        round_x(nc.scalar.copy, 0, 0, SPLIT[0])
-        round_x(nc.vector.tensor_copy, 0, SPLIT[0], M)
         for b in range(2):
             sign_first_half(b, halves[b])
         quantise_x(0)
-        quantise_wd(0)
-        round_x(nc.scalar.copy, 1, 0, M // 4)
-        round_x(nc.scalar.copy, 1, M // 4, M // 2)
-        round_x(nc.vector.tensor_copy, 1, M // 2, M)
-        for lo, hi in ((0, M // 4), (M // 2, M), (M // 4, M // 2)):
-            nc.vector.quantize_mx(x_w[1][:, lo:hi].bitcast(FP8X4), x_s[1][:, lo:hi], x_bf[1][:, lo:hi, :].rearrange("p c t -> p (c t)"))
-        rectify_rows("next", 1, RAW * 5 + RAW // 2)
+        rectify_rows("next", 1)
         weave_h("next", 0)
+        pick_and_turn_halves(1)
+        quantise_h("next", 0, None)
+        quantise_wd(0, ROWS["next", 0] + 2048)
+        sign_wd(1, ROWS["next", 0])
+        for half in range(2):
+            lo, hi = M // 2 * half, M // 2 * (half + 1)
+            round_x(nc.scalar.copy, 1, lo, hi)
+            nc.vector.quantize_mx(x_w[1][:, lo:hi].bitcast(FP8X4), x_s[1][:, lo:hi], x_bf[1][:, lo:hi, :].rearrange("p c t -> p (c t)"))
+        quantise_wd(1, RAW * 5)
         weave_h("next", 1)
         hidden("now", 0)
         hidden("now", 1, (0, 2))
-        rectify("now", 0)
-        join_h(nc.scalar.copy, "now", 0)
+        rectify_rows("now", 0)
         hidden("now", 1, (1, 3))
-        rectify("now", 1, (0,))
-        for i in (1, 2):
-            pick_wd(i)
-            turn_wd(i)
-        last_wd()
-        rectify("now", 1, (2, 1, 3))
+        weave_h("now", 0)
+        rectify("now", 1)
         join_h(nc.scalar.copy, "now", 1)
-        quantise_h("next", 0, LAST_PICKED - 448)
-        quantise_h("next", 1, LAST_PICKED + 128)
-        sign_wd(1, LAST_PICKED + 960)
-        sign_wd(2, ROUNDED_H["next", 0])
-        quantise_wd(1)
-        sign_wd(3, None)
+        pick_wd(2, ROUNDED_X[1])
+        turn_wd(2)
+        for i in range(2):
+            down("next", i, (0,))
+        pick_and_turn_halves(3)
+        sign_wd(2, PICKED_HALVES[3][0] - 2048 + 64)
+        quantise_h("next", 1, PICKED_HALVES[3][0] + 512)
         quantise_wd(2)
+        sign_wd(3, ROWS["now", 0])
+        quantise_h("now", 0, None)
         quantise_wd(3)
-        quantise_h("now", 0, ROUNDED_H["next", 1])
         quantise_h("now", 1, None)
-        discount_aside(0, 0, ROUNDED_H["now", 0])
-        discount_aside(1, 2048, ROUNDED_H["now", 1])
-        discount(2, 4096)
-        discount(3, 6144)
+        for i in range(2):
+            down("next", i, (1,))
+        down("next", 2)
+        down("now", 2, (0,))
+        down("next", 3)
+        down("now", 3, (0,))
+        for i in (2, 3):
+            down("now", i, (1,))
+        for i in range(2):
+            down("now", i, (1, 0))
+        for i in range(2):
+            discount_aside(i)
+        for i in (2, 3):
+            discount(i)
         for i in (2, 3, 0):
             finish(i)
         finish(1, 2)

@@ -23,11 +23,11 @@ KIB = 1024
 AHEAD = 3 * T // 4
 FIRST_BANKS = (0, 2)
 ROUNDED_X = (48 * KIB, 92 * KIB)
-PICKED_HALVES = {1: (RAW * 4, RAW * 4 + 1024), 3: (62 * KIB, 63 * KIB)}
+PICKED_HALVES = {1: (56 * KIB, 58 * KIB), 3: (62 * KIB, 63 * KIB)}
 PAIRS = 68 * KIB
-ROWS = {("next", 0): 104 * KIB, ("next", 1): RAW * 4 + 4096, ("now", 0): 112 * KIB}
-ROUNDED_H = {("next", 0): ROUNDED_X[0], ("next", 1): 104 * KIB - 4096 + 64, ("now", 0): 76 * KIB, ("now", 1): 80 * KIB}
-HIDDEN_BANKS = {"next": (0, 1, 2, 3, 4, 5, 6, 7), "now": (1, 4, 3, 6, 5, 4, 7, 6)}
+ROWS = {("next", 0): 108 * KIB, ("next", 1): 116 * KIB, ("now", 0): 112 * KIB}
+ROUNDED_H = {("next", 0): 120 * KIB, ("next", 1): 104 * KIB, ("now", 0): 76 * KIB, ("now", 1): 80 * KIB}
+HIDDEN_BANKS = {"next": (0, 1, 2, 3, 4, 0, 6, 2), "now": (1, 4, 3, 6, 5, 4, 7, 6)}
 TURN_BANKS = (0, 2, 0, 2)
 DOWN_BANKS = {"next": (4, 6, 1, 3), "now": (5, 7, 0, 2)}
 
@@ -89,8 +89,8 @@ def tile_list_sparse_td_features_kernel(tc, tab_words, tab_scales, offs, x, xn_w
             v_s[4:116, :, :].rearrange("p t c -> p (t c)").bitcast(I32),
         )
         nc.sync.dma_start(wd_raw[0][:, AHEAD:T], wdT[0:P, AHEAD:T])
-        nc.sync.dma_start(x_raw[0][:], x_rows[0])
         nc.sync.dma_start(wd_raw[1][:], wdT[P : 2 * P, :])
+        nc.sync.dma_start(x_raw[0][:], x_rows[0])
         nc.sync.dma_start(x_raw[1][:], x_rows[1])
         for i in range(2, 4):
             nc.sync.dma_start(wd_raw[i][:], wdT[P * i : P * (i + 1), :])
@@ -107,7 +107,15 @@ def tile_list_sparse_td_features_kernel(tc, tab_words, tab_scales, offs, x, xn_w
         gain = keep.tile([P, 2, 4], F32, name="gain")
         sign0 = keep.tile([P, 2, 4], F32, name="sign0")
         sign = keep.tile([P, 2, 4], BF16, name="sign")
-        nc.scalar.activation(gain[:], g_cols, ACT.Abs)
+        g_odd = keep.tile([P, 2], F32, name="g_odd")
+        gain_odd = arena.tile([P, 2], F32, name="gain_odd", align_bytes=64, offset=RAW * 5 + 6144)
+        nc.scalar.activation(gain[:, 0, :], g_cols[:, 0, :], ACT.Abs)
+        nc.scalar.activation(gain[:, 1, 0:4:2], g_cols[:, 1, 0:4:2], ACT.Abs)
+        nc.scalar.copy(g_odd[:], g_cols[:, 1, 1:4:2])
+
+        def gain_of(b, t):
+            return gain_odd[:, t // 2 : t // 2 + 1] if b == 1 and t % 2 == 1 else gain[:, b, t : t + 1]
+
         nc.scalar.activation(sign0[:], g_cols, ACT.Sign)
         nc.scalar.activation(sign[:], sign0[:], ACT.Sign, bias=0.5)
 
@@ -127,10 +135,6 @@ def tile_list_sparse_td_features_kernel(tc, tab_words, tab_scales, offs, x, xn_w
                 x_raw[a][:, :, cols].rearrange("p t (c i) -> p c t i", i=4),
             )
 
-        def round_x_aside(a, half):
-            cols = slice(M // 2 * half, M // 2 * (half + 1))
-            nc.gpsimd.tensor_scalar(x_bf[a][:, cols, :], x_raw[a][:, :, cols].rearrange("p t c -> p c t"), 1.0, 0.0, ALU.mult, ALU.add)
-
         def quantise_x(a):
             nc.vector.quantize_mx(x_w[a][:].bitcast(FP8X4), x_s[a][:], x_bf[a][:].rearrange("p c t -> p (c t)"))
 
@@ -140,7 +144,7 @@ def tile_list_sparse_td_features_kernel(tc, tab_words, tab_scales, offs, x, xn_w
             for t in codes:
                 acc = psum.tile([P, M], F32, name="acc", tag="bank%d" % HIDDEN_BANKS[side][4 * b + t])
                 cols = slice(P * b, P * (b + 1))
-                early = (b == 0 and t % 2 == 0) if side == "next" else True
+                early = (b == 0 and t % 2 == 0) if side == "next" else b == 0
                 passes = (0, 1) if early else (1, 0)
                 for a in passes:
                     words = v_w0[:, t, cols] if a == 0 else v_w1[b][:, t, :]
@@ -161,12 +165,13 @@ def tile_list_sparse_td_features_kernel(tc, tab_words, tab_scales, offs, x, xn_w
             if (side, b) not in h_pairs:
                 h_pairs[side, b] = arena.tile([P, 2, M, 2], BF16, name="pairs", align_bytes=64, offset=PAIRS)
             for t in codes:
-                nc.scalar.activation(h_pairs[side, b][:, t // 2, :, t % 2], sums[side, b, t][:], ACT.Relu, scale=gain[:, b, t : t + 1])
+                nc.scalar.activation(h_pairs[side, b][:, t // 2, :, t % 2], sums[side, b, t][:], ACT.Relu, scale=gain_of(b, t))
 
-        def rectify_rows(side, b):
-            h_pairs[side, b] = arena.tile([P, 4, M], BF16, name="h_rows_%s%d" % (side, b), align_bytes=64, offset=ROWS[side, b])
-            for t in (0, 2, 1, 3):
-                nc.scalar.activation(h_pairs[side, b][:, t, :], sums[side, b, t][:], ACT.Relu, scale=gain[:, b, t : t + 1])
+        def rectify_rows(side, b, codes=(0, 2, 1, 3)):
+            if (side, b) not in h_pairs:
+                h_pairs[side, b] = arena.tile([P, 4, M], BF16, name="h_rows_%s%d" % (side, b), align_bytes=64, offset=ROWS[side, b])
+            for t in codes:
+                nc.scalar.activation(h_pairs[side, b][:, t, :], sums[side, b, t][:], ACT.Relu, scale=gain_of(b, t))
 
         def weave_h(side, b):
             h_bf[side, b] = arena.tile([P, M, 4], BF16, name="h_bf_%s%d" % (side, b), align_bytes=64, offset=ROUNDED_H[side, b])
@@ -224,28 +229,6 @@ def tile_list_sparse_td_features_kernel(tc, tab_words, tab_scales, offs, x, xn_w
                 for u in range(2):
                     nc.tensor.transpose(turned[:, u, b, :], words[:, u, :], ident[:])
 
-        def first_wd_half(b):
-            picked = keep.tile([P, 2, P, 2], BF16, name="first_picked%d" % b)
-            nc.vector.tensor_copy(picked[:].rearrange("p u (c r) e -> p c u e r", r=8), wd_raw[0][:].indirect(offsets[:, 32 * b : 32 * (b + 1)]))
-            return picked
-
-        def turn_first_half(b, picked):
-            words = picked[:].rearrange("p u c e -> p u (c e)").bitcast(F32)
-            turned = psum.tile([P, 2, P], F32, name="first_turned", tag="bank%d" % FIRST_BANKS[b])
-            for u in range(2):
-                nc.tensor.transpose(turned[:, u, :], words[:, u, :], ident[:])
-            return turned
-
-        def sign_first_half(b, turned):
-            if b == 0:
-                wd_bf[0] = keep.tile([P, 2 * P, 4], BF16, name="wd_bf0", align_bytes=64)
-            nc.vector.tensor_tensor(
-                wd_bf[0][:, P * b : P * (b + 1), :].rearrange("p n (u e) -> p n u e", e=2),
-                turned[:].bitcast(BF16).rearrange("p u (n e) -> p n u e", e=2),
-                sign[:, b, :].rearrange("p (u e) -> p u e", e=2).unsqueeze(1).to_broadcast([P, P, 2, 2]),
-                ALU.mult,
-            )
-
         def quantise_wd(i, place=None):
             if place is None:
                 wd_w[i] = keep.tile([P, 2 * P], U32, name="wd_w%d" % i, align_bytes=64)
@@ -277,11 +260,14 @@ def tile_list_sparse_td_features_kernel(tc, tab_words, tab_scales, offs, x, xn_w
             discounted[i] = discounted_late[:, i - 2, :]
             nc.vector.tensor_tensor(discounted[i], sums_down["next", i][:], gam_row[:], ALU.mult)
 
-        def discount_aside(i):
+        def discount_aside(i, pieces):
             nc.scalar.copy(copied[:, i, :], sums_down["next", i][:])
             aside = arena.tile([P, M], F32, name="discounted%d" % i, align_bytes=64, offset=ROUNDED_H["now", i])
             discounted[i] = aside[:]
-            nc.gpsimd.tensor_tensor(discounted[i], copied[:, i, :], gam_row[:], ALU.mult)
+            width = M // pieces
+            for piece in range(pieces):
+                cols = slice(width * piece, width * (piece + 1))
+                nc.gpsimd.tensor_tensor(aside[:, cols], copied[:, i, cols], gam_row[:, cols], ALU.mult)
 
         def finish(i, pieces=1):
             y = sums_down["now", i]
@@ -292,27 +278,29 @@ def tile_list_sparse_td_features_kernel(tc, tab_words, tab_scales, offs, x, xn_w
                 nc.vector.tensor_tensor(result[:], discounted[i][:, cols], y[:, cols], ALU.subtract)
                 nc.sync.dma_start(out[P * i : P * (i + 1), cols], result[:])
 
-        round_x(nc.scalar.copy, 0, 0, M // 2)
-        round_x_aside(0, 1)
         hidden("next", 0)
         rectify_rows("next", 0)
-        halves = [first_wd_half(b) for b in range(2)]
         hidden("next", 1, (0, 2))
-        halves = [turn_first_half(b, halves[b]) for b in range(2)]
-        hidden("next", 1, (1, 3))
-        for b in range(2):
-            sign_first_half(b, halves[b])
-        quantise_x(0)
-        rectify_rows("next", 1)
+        rectify_rows("next", 1, (0, 2))
         weave_h("next", 0)
+        pick_wd(0, 84 * KIB)
+        turn_wd(0)
         pick_and_turn_halves(1)
+        sign_wd(0, PICKED_HALVES[1][0])
+        sign_wd(1, 104 * KIB)
+        hidden("next", 1, (1, 3))
+        round_x(nc.scalar.copy, 0, 0, M)
+        quantise_wd(0)
         quantise_h("next", 0, None)
-        quantise_wd(0, ROWS["next", 0] + 2048)
-        sign_wd(1, ROWS["next", 0])
+        quantise_x(0)
+        round_x(nc.vector.tensor_copy, 1, 5 * M // 8, M)
+        round_x(nc.scalar.copy, 1, 0, M // 2)
+        round_x(nc.scalar.copy, 1, M // 2, 5 * M // 8)
         for half in range(2):
             lo, hi = M // 2 * half, M // 2 * (half + 1)
-            round_x(nc.scalar.copy, 1, lo, hi)
             nc.vector.quantize_mx(x_w[1][:, lo:hi].bitcast(FP8X4), x_s[1][:, lo:hi], x_bf[1][:, lo:hi, :].rearrange("p c t -> p (c t)"))
+        nc.scalar.activation(gain_odd[:], g_odd[:], ACT.Abs)
+        rectify_rows("next", 1, (1, 3))
         quantise_wd(1, RAW * 5)
         weave_h("next", 1)
         hidden("now", 0)
@@ -328,24 +316,24 @@ def tile_list_sparse_td_features_kernel(tc, tab_words, tab_scales, offs, x, xn_w
             down("next", i, (0,))
         pick_and_turn_halves(3)
         sign_wd(2, PICKED_HALVES[3][0] - 2048 + 64)
+        sign_wd(3, None)
         quantise_h("next", 1, PICKED_HALVES[3][0] + 512)
         quantise_wd(2)
-        sign_wd(3, ROWS["now", 0])
-        quantise_h("now", 0, None)
         quantise_wd(3)
+        quantise_h("now", 0, None)
         quantise_h("now", 1, None)
         for i in range(2):
             down("next", i, (1,))
         down("next", 2)
-        down("now", 2, (0,))
         down("next", 3)
-        down("now", 3, (0,))
+        for i in (2, 3):
+            down("now", i, (0,))
         for i in (2, 3):
             down("now", i, (1,))
         for i in range(2):
             down("now", i, (1, 0))
         for i in range(2):
-            discount_aside(i)
+            discount_aside(i, i + 1)
         for i in (2, 3):
             discount(i)
         for i in (2, 3, 0):

@@ -66,8 +66,8 @@ def tile_list_sparse_td_features_kernel(tc, tab_words, tab_scales, offs, x, xn_w
 
         nc.sync.dma_start(offsets[:], offs)
         nc.sync.dma_start(xn_w[:].bitcast(I32), xn_words.rearrange("a p c -> p a c").bitcast(I32))
-        for q in (0, 2, 1, 3):
-            nc.sync.dma_start(tab_s[32 * q : 32 * q + 8, :].bitcast(I32), tab_scales[:, 4 * q : 4 * q + 4, :].bitcast(I32))
+        for r in range(4):
+            nc.sync.dma_start(tab_s[r:P:16, :].bitcast(I32), tab_scales[:, r:16:4, :].rearrange("a q c -> q a c").bitcast(I32))
         for a in range(2):
             nc.sync.dma_start(tab_w[a][:].bitcast(I32), tab_words[a].rearrange("p t i -> p (t i)").bitcast(I32))
         nc.sync.dma_start(gam_cols[:], gam.rearrange("(p c) -> p c", c=4))
@@ -86,7 +86,7 @@ def tile_list_sparse_td_features_kernel(tc, tab_words, tab_scales, offs, x, xn_w
         nc.sync.dma_start(wd_raw[0][:, 0:AHEAD], wdT[0:P, 0:AHEAD])
         nc.sync.dma_start(
             v_s1[0:112, :, :].rearrange("p t c -> p (t c)").bitcast(I32),
-            v_s[4:116, :, :].rearrange("p t c -> p (t c)").bitcast(I32),
+            v_s[16:P, :, :].rearrange("p t c -> p (t c)").bitcast(I32),
         )
         nc.sync.dma_start(wd_raw[0][:, AHEAD:T], wdT[0:P, AHEAD:T])
         nc.sync.dma_start(wd_raw[1][:], wdT[P : 2 * P, :])
@@ -150,10 +150,8 @@ def tile_list_sparse_td_features_kernel(tc, tab_words, tab_scales, offs, x, xn_w
                     words = v_w0[:, t, cols] if a == 0 else v_w1[b][:, t, :]
                     if a == 0:
                         plane = v_s[:, t, cols]
-                    elif side == "next":
-                        plane = v_s1[:, t, cols]
                     else:
-                        plane = v_s[4:P, t, cols]
+                        plane = v_s1[:, t, cols]
                     if side == "next":
                         rhs, rhs_scale = xn_w[:, a, :].bitcast(FP4X4), xn_s[:, a, :]
                     else:

@@ -173,7 +173,11 @@ def tile_list_sparse_td_features_kernel(tc, tab_words, tab_scales, offs, x, xn_w
 
         def weave_h(side, b):
             h_bf[side, b] = arena.tile([P, M, 4], BF16, name="h_bf_%s%d" % (side, b), align_bytes=64, offset=ROUNDED_H[side, b])
-            nc.gpsimd.tensor_scalar(h_bf[side, b][:], h_pairs[side, b][:].rearrange("p t m -> p m t"), 1.0, 0.0, ALU.mult, ALU.add)
+            nc.gpsimd.tensor_scalar(
+                h_bf[side, b][:].rearrange("p (c i) t -> p c t i", i=4),
+                h_pairs[side, b][:].rearrange("p t (c i) -> p c t i", i=4),
+                1.0, 0.0, ALU.mult, ALU.add,
+            )
 
         def join_h(copy, side, b):
             h_bf[side, b] = arena.tile([P, M, 4], BF16, name="h_bf_%s%d" % (side, b), align_bytes=64, offset=ROUNDED_H[side, b])

@@ -20,16 +20,17 @@ ACT = mybir.ActivationFunctionType
 P = 128
 RAW = T * 4
 KIB = 1024
-AHEAD = 3 * T // 4
-FIRST_BANKS = (0, 2)
+AHEAD = T // 2
 ROUNDED_X = (48 * KIB, 92 * KIB)
 PICKED_HALVES = {1: (56 * KIB, 58 * KIB), 3: (62 * KIB, 63 * KIB)}
 PAIRS = 68 * KIB
+SIGNED_LAST = 124 * KIB
 ROWS = {("next", 0): 108 * KIB, ("next", 1): 116 * KIB, ("now", 0): 112 * KIB}
 ROUNDED_H = {("next", 0): 120 * KIB, ("next", 1): 104 * KIB, ("now", 0): 76 * KIB, ("now", 1): 80 * KIB}
-HIDDEN_BANKS = {"next": (0, 1, 2, 3, 4, 0, 6, 2), "now": (1, 4, 3, 6, 5, 4, 7, 6)}
-TURN_BANKS = (0, 2, 0, 2)
-DOWN_BANKS = {"next": (4, 6, 1, 3), "now": (5, 7, 0, 2)}
+HIDDEN_BANKS = {"next": (0, 1, 2, 3, 4, 0, 6, 2), "now": (1, 4, 3, 6, 5, 4, 7, 5)}
+TURN_BANKS = {0: 0, 2: 0}
+HALF_TURN_BANKS = {1: (2, 5), 3: (2, 7)}
+DOWN_BANKS = {"next": (4, 5, 1, 3), "now": (6, 7, 0, 2)}
 
 
 def tile_list_sparse_td_features_kernel(tc, tab_words, tab_scales, offs, x, xn_words, xn_scales, g, wdT, gam, out):
@@ -44,7 +45,6 @@ def tile_list_sparse_td_features_kernel(tc, tab_words, tab_scales, offs, x, xn_w
         tab_w = [keep.tile([P, T], U32, name="tab_w%d" % a, align_bytes=64) for a in range(2)]
         xn_w = keep.tile([P, 2, 2 * M], U8, name="xn_w", align_bytes=64)
         xn_s = keep.tile([P, 2, M], U8, name="xn_s", align_bytes=64)
-        v_s_listed = keep.tile([P, S], U8, name="v_s_listed", align_bytes=64)
         v_s = keep.tile([P, 4, 2 * P], U8, name="v_s", align_bytes=64)
         v_s1 = keep.tile([P, 4, 2 * P], U8, name="v_s1", align_bytes=64)
         v_w0 = keep.tile([P, 4, 2 * P], U32, name="v_w0", align_bytes=64)
@@ -68,20 +68,13 @@ def tile_list_sparse_td_features_kernel(tc, tab_words, tab_scales, offs, x, xn_w
         nc.sync.dma_start(xn_w[:].bitcast(I32), xn_words.rearrange("a p c -> p a c").bitcast(I32))
         for r in range(4):
             nc.sync.dma_start(tab_s[r:P:16, :].bitcast(I32), tab_scales[:, r:16:4, :].rearrange("a q c -> q a c").bitcast(I32))
-        for a in range(2):
-            nc.sync.dma_start(tab_w[a][:].bitcast(I32), tab_words[a].rearrange("p t i -> p (t i)").bitcast(I32))
+        nc.sync.dma_start(tab_w[0][:].bitcast(I32), tab_words[0].rearrange("p t i -> p (t i)").bitcast(I32))
         nc.sync.dma_start(gam_cols[:], gam.rearrange("(p c) -> p c", c=4))
+        nc.sync.dma_start(tab_w[1][:].bitcast(I32), tab_words[1].rearrange("p t i -> p (t i)").bitcast(I32))
         for r in range(4):
             nc.sync.dma_start(xn_s[r:P:32, :, :].bitcast(I32), xn_scales[:, r:16:4, :].rearrange("a q c -> q a c").bitcast(I32))
 
-        parts = ((0, 3 * S // 4), (3 * S // 4, S))
-        for lo, hi in parts:
-            nc.vector.tensor_copy(v_s_listed[:, lo:hi], tab_s[:].indirect(offsets[:, lo // 16 : hi // 16]))
-        for lo, hi in parts:
-            nc.vector.tensor_copy(
-                v_s[:, :, lo // 4 : hi // 4].bitcast(I32).rearrange("p t (c w) -> p t c w", w=2),
-                v_s_listed[:, lo:hi].bitcast(I32).rearrange("p (c t w) -> p t c w", t=4, w=2),
-            )
+        nc.vector.tensor_copy(v_s[:].rearrange("p t (c r) -> p c t r", r=8), tab_s[:].indirect(offsets[:]))
         x_rows = [x[512 * a : 512 * (a + 1), :].rearrange("(p j) m -> p j m", j=4) for a in range(2)]
         nc.sync.dma_start(wd_raw[0][:, 0:AHEAD], wdT[0:P, 0:AHEAD])
         nc.sync.dma_start(
@@ -209,27 +202,33 @@ def tile_list_sparse_td_features_kernel(tc, tab_words, tab_scales, offs, x, xn_w
                 for u in range(2):
                     nc.tensor.transpose(turned[:, u, b, :], words[:, u, P * b : P * (b + 1)], ident[:])
 
+        def sign_halves(i, place):
+            wd_bf[i] = arena.tile([P, 2 * P, 4], BF16, name="wd_bf%d" % i, align_bytes=64, offset=place)
+            for b in range(2):
+                nc.vector.tensor_tensor(
+                    wd_bf[i][:, P * b : P * (b + 1), :].rearrange("p n (u e) -> p n u e", e=2),
+                    wd_turned[i, b][:].bitcast(BF16).rearrange("p u (n e) -> p n u e", e=2),
+                    sign[:, b, :].rearrange("p (u e) -> p u e", e=2).unsqueeze(1).to_broadcast([P, P, 2, 2]),
+                    ALU.mult,
+                )
+
+        def pick_and_turn_apart(i):
+            for b in range(2):
+                wd_turned[i, b] = psum.tile([P, 2, P], F32, name="turned", tag="bank%d" % HALF_TURN_BANKS[i][b])
+                picked = arena.tile([P, 2, P, 2], BF16, name="picked%d_%d" % (i, b), align_bytes=64, offset=PICKED_HALVES[i][b])
+                nc.vector.tensor_copy(picked[:].rearrange("p u (c r) e -> p c u e r", r=8), wd_raw[i][:].indirect(offsets[:, 32 * b : 32 * (b + 1)]))
+                words = picked[:].rearrange("p u c e -> p u (c e)").bitcast(F32)
+                for u in range(2):
+                    nc.tensor.transpose(wd_turned[i, b][:, u, :], words[:, u, :], ident[:])
+
         def sign_wd(i, place):
-            if place is None:
-                wd_bf[i] = keep.tile([P, 2 * P, 4], BF16, name="wd_bf%d" % i, align_bytes=64)
-            else:
-                wd_bf[i] = arena.tile([P, 2 * P, 4], BF16, name="wd_bf%d" % i, align_bytes=64, offset=place)
+            wd_bf[i] = arena.tile([P, 2 * P, 4], BF16, name="wd_bf%d" % i, align_bytes=64, offset=place)
             nc.vector.tensor_tensor(
                 wd_bf[i][:].rearrange("p (b n) (u e) -> p b n u e", b=2, e=2),
                 wd_turned[i][:].bitcast(BF16).rearrange("p u b (n e) -> p b n u e", e=2),
                 sign[:].rearrange("p b (u e) -> p b u e", e=2).unsqueeze(2).to_broadcast([P, 2, P, 2, 2]),
                 ALU.mult,
             )
-
-        def pick_and_turn_halves(i):
-            turned = psum.tile([P, 2, 2, P], F32, name="turned", tag="bank%d" % TURN_BANKS[i])
-            wd_turned[i] = turned
-            for b in range(2):
-                picked = arena.tile([P, 2, P, 2], BF16, name="picked%d_%d" % (i, b), align_bytes=64, offset=PICKED_HALVES[i][b])
-                nc.vector.tensor_copy(picked[:].rearrange("p u (c r) e -> p c u e r", r=8), wd_raw[i][:].indirect(offsets[:, 32 * b : 32 * (b + 1)]))
-                words = picked[:].rearrange("p u c e -> p u (c e)").bitcast(F32)
-                for u in range(2):
-                    nc.tensor.transpose(turned[:, u, b, :], words[:, u, :], ident[:])
 
         def quantise_wd(i, place=None):
             if place is None:
@@ -256,15 +255,15 @@ def tile_list_sparse_td_features_kernel(tc, tab_words, tab_scales, offs, x, xn_w
 
         discounted = {}
         copied = arena.tile([P, 2, M], F32, name="copied", align_bytes=64, offset=PAIRS - 4096 + 64)
-        discounted_late = arena.tile([P, 2, M], F32, name="discounted_late", align_bytes=64, offset=PAIRS + 4096 - 64)
 
-        def discount(i):
-            discounted[i] = discounted_late[:, i - 2, :]
+        def discount(i, place):
+            late = arena.tile([P, M], F32, name="discounted%d" % i, align_bytes=64, offset=place)
+            discounted[i] = late[:]
             nc.vector.tensor_tensor(discounted[i], sums_down["next", i][:], gam_row[:], ALU.mult)
 
         def discount_aside(i, pieces):
             nc.scalar.copy(copied[:, i, :], sums_down["next", i][:])
-            aside = arena.tile([P, M], F32, name="discounted%d" % i, align_bytes=64, offset=ROUNDED_H["now", i])
+            aside = arena.tile([P, M], F32, name="discounted%d" % i, align_bytes=64, offset=ROUNDED_H["now", 1] + 2 * KIB * i)
             discounted[i] = aside[:]
             width = M // pieces
             for piece in range(pieces):
@@ -287,13 +286,13 @@ def tile_list_sparse_td_features_kernel(tc, tab_words, tab_scales, offs, x, xn_w
         weave_h("next", 0)
         pick_wd(0, 84 * KIB)
         turn_wd(0)
-        pick_and_turn_halves(1)
+        pick_and_turn_apart(1)
         sign_wd(0, PICKED_HALVES[1][0])
-        sign_wd(1, 104 * KIB)
+        sign_halves(1, ROUNDED_H["next", 1])
+        quantise_h("next", 0, None)
         hidden("next", 1, (1, 3))
         round_x(nc.scalar.copy, 0, 0, M)
-        quantise_wd(0)
-        quantise_h("next", 0, None)
+        quantise_wd(0, ROWS["next", 0] + 2 * KIB)
         quantise_x(0)
         round_x(nc.vector.tensor_copy, 1, 5 * M // 8, M)
         round_x(nc.scalar.copy, 1, 0, M // 2)
@@ -316,28 +315,27 @@ def tile_list_sparse_td_features_kernel(tc, tab_words, tab_scales, offs, x, xn_w
         turn_wd(2)
         for i in range(2):
             down("next", i, (0,))
-        pick_and_turn_halves(3)
+        pick_and_turn_apart(3)
         sign_wd(2, PICKED_HALVES[3][0] - 2048 + 64)
-        sign_wd(3, None)
-        quantise_h("next", 1, PICKED_HALVES[3][0] + 512)
-        quantise_wd(2)
-        quantise_wd(3)
+        sign_halves(3, SIGNED_LAST)
+        quantise_h("next", 1, ROWS["now", 0])
+        quantise_wd(2, ROWS["now", 0] + KIB)
         quantise_h("now", 0, None)
+        quantise_wd(3, ROWS["now", 0] + 2 * KIB)
         quantise_h("now", 1, None)
         for i in range(2):
             down("next", i, (1,))
         down("next", 2)
+        down("now", 2, (0,))
         down("next", 3)
-        for i in (2, 3):
-            down("now", i, (0,))
-        for i in (2, 3):
-            down("now", i, (1,))
+        down("now", 2, (1,))
+        down("now", 3)
         for i in range(2):
             down("now", i, (1, 0))
         for i in range(2):
             discount_aside(i, i + 1)
-        for i in (2, 3):
-            discount(i)
+        discount(2, PAIRS + 4096 - 64)
+        discount(3, PAIRS + 64)
         for i in (2, 3, 0):
             finish(i)
         finish(1, 2)

@@ -20,6 +20,7 @@ ACT = mybir.ActivationFunctionType
 P = 128
 RAW = T * 4
 KIB = 1024
+DMA_ALIGN = 256
 AHEAD = T // 2
 ROUNDED_X = (48 * KIB, 92 * KIB)
 PICKED_HALVES = {1: (56 * KIB, 58 * KIB), 3: (62 * KIB, 63 * KIB)}
@@ -41,19 +42,19 @@ def tile_list_sparse_td_features_kernel(tc, tab_words, tab_scales, offs, x, xn_w
         psum = ctx.enter_context(tc.psum_pool(name="psum", bufs=1))
 
         offsets = keep.tile([P, S // 16], U16, name="offsets")
-        tab_s = keep.tile([P, T], U8, name="tab_s", align_bytes=64)
-        tab_w = [keep.tile([P, T], U32, name="tab_w%d" % a, align_bytes=64) for a in range(2)]
-        xn_w = keep.tile([P, 2, 2 * M], U8, name="xn_w", align_bytes=64)
-        xn_s = keep.tile([P, 2, M], U8, name="xn_s", align_bytes=64)
-        v_s = keep.tile([P, 4, 2 * P], U8, name="v_s", align_bytes=64)
-        v_s1 = keep.tile([P, 4, 2 * P], U8, name="v_s1", align_bytes=64)
+        tab_s = keep.tile([P, T], U8, name="tab_s", align_bytes=DMA_ALIGN)
+        tab_w = [keep.tile([P, T], U32, name="tab_w%d" % a, align_bytes=DMA_ALIGN) for a in range(2)]
+        xn_w = keep.tile([P, 2, 2 * M], U8, name="xn_w", align_bytes=DMA_ALIGN)
+        xn_s = keep.tile([P, 2, M], U8, name="xn_s", align_bytes=DMA_ALIGN)
+        v_s = keep.tile([P, 4, 2 * P], U8, name="v_s", align_bytes=DMA_ALIGN)
+        v_s1 = keep.tile([P, 4, 2 * P], U8, name="v_s1", align_bytes=DMA_ALIGN)
         v_w0 = keep.tile([P, 4, 2 * P], U32, name="v_w0", align_bytes=64)
         v_w1 = [keep.tile([P, 4, P], U32, name="v_w1_%d" % b, align_bytes=64) for b in range(2)]
         g_raw = keep.tile([2, 4 * P], F32, name="g_raw")
         rows = keep.tile([P, 4, P], F32, name="rows")
         ident = keep.tile([P, P], F32, name="ident")
-        wd_raw = [arena.tile([P, T], F32, name="wd_raw%d" % i, align_bytes=64, offset=RAW * i) for i in range(4)]
-        x_raw = [arena.tile([P, 4, M], F32, name="x_raw%d" % a, align_bytes=64, offset=RAW * (4 + a)) for a in range(2)]
+        wd_raw = [arena.tile([P, T], F32, name="wd_raw%d" % i, align_bytes=DMA_ALIGN, offset=RAW * i) for i in range(4)]
+        x_raw = [arena.tile([P, 4, M], F32, name="x_raw%d" % a, align_bytes=DMA_ALIGN, offset=RAW * (4 + a)) for a in range(2)]
         gam_row = keep.tile([P, M], F32, name="gam_row")
         gam_cols = keep.tile([P, 4], F32, name="gam_cols")
 
@@ -275,7 +276,7 @@ def tile_list_sparse_td_features_kernel(tc, tab_words, tab_scales, offs, x, xn_w
             width = M // pieces
             for piece in range(pieces):
                 cols = slice(width * piece, width * (piece + 1))
-                result = keep.tile([P, width], F32, name="result%d_%d" % (i, piece))
+                result = keep.tile([P, width], F32, name="result%d_%d" % (i, piece), align_bytes=DMA_ALIGN)
                 nc.vector.tensor_tensor(result[:], discounted[i][:, cols], y[:, cols], ALU.subtract)
                 nc.sync.dma_start(out[P * i : P * (i + 1), cols], result[:])
 

from contextlib import ExitStack

import concourse.mybir as mybir
from concourse.masks import make_identity

K, T, S, M, N = 1024, 2048, 1024, 512, 512
FLOPS = 2 * K * S * 2 * M + 2 * S * N * 2 * M

F32 = mybir.dt.float32
BF16 = mybir.dt.bfloat16
I32 = mybir.dt.int32
U32 = mybir.dt.uint32
U16 = mybir.dt.uint16
U8 = mybir.dt.uint8
FP8X4 = mybir.dt.float8_e4m3fn_x4
FP4X4 = mybir.dt.float4_e2m1fn_x4
ALU = mybir.AluOpType
ACT = mybir.ActivationFunctionType

P = 128
RAW = T * 4
KIB = 1024
DMA_ALIGN = 256
AHEAD = T // 2
ROUNDED_X = (48 * KIB, 92 * KIB)
PICKED_HALVES = {1: (56 * KIB, 58 * KIB), 3: (62 * KIB, 63 * KIB)}
PAIRS = 68 * KIB
SIGNED_LAST = 124 * KIB
ROWS = {("next", 0): 108 * KIB, ("next", 1): 116 * KIB, ("now", 0): 112 * KIB}
ROUNDED_H = {("next", 0): 120 * KIB, ("next", 1): 104 * KIB, ("now", 0): 76 * KIB, ("now", 1): 80 * KIB}
HIDDEN_BANKS = {"next": (0, 1, 2, 3, 4, 0, 6, 2), "now": (1, 4, 3, 6, 5, 4, 7, 5)}
TURN_BANKS = {0: 0, 2: 0}
HALF_TURN_BANKS = {1: (2, 5), 3: (2, 7)}
DOWN_BANKS = {"next": (4, 5, 1, 3), "now": (6, 7, 0, 2)}


def tile_list_sparse_td_features_kernel(tc, tab_words, tab_scales, offs, x, xn_words, xn_scales, g, wdT, gam, out):
    nc = tc.nc
    with ExitStack() as ctx:
        keep = ctx.enter_context(tc.tile_pool(name="keep", bufs=1))
        arena = ctx.enter_context(tc.tile_pool(name="arena", bufs=1))
        psum = ctx.enter_context(tc.psum_pool(name="psum", bufs=1))

        offsets = keep.tile([P, S // 16], U16, name="offsets")
        tab_s = keep.tile([P, T], U8, name="tab_s", align_bytes=DMA_ALIGN)
        tab_w = [keep.tile([P, T], U32, name="tab_w%d" % a, align_bytes=DMA_ALIGN) for a in range(2)]
        xn_w = keep.tile([P, 2, 2 * M], U8, name="xn_w", align_bytes=DMA_ALIGN)
        xn_s = keep.tile([P, 2, M], U8, name="xn_s", align_bytes=DMA_ALIGN)
        v_s = keep.tile([P, 4, 2 * P], U8, name="v_s", align_bytes=DMA_ALIGN)
        v_s1 = keep.tile([P, 4, 2 * P], U8, name="v_s1", align_bytes=DMA_ALIGN)
        v_w0 = keep.tile([P, 4, 2 * P], U32, name="v_w0", align_bytes=64)
        v_w1 = [keep.tile([P, 4, P], U32, name="v_w1_%d" % b, align_bytes=64) for b in range(2)]
        g_raw = keep.tile([2, 4 * P], F32, name="g_raw")
        rows = keep.tile([P, 4, P], F32, name="rows")
        ident = keep.tile([P, P], F32, name="ident")
        wd_raw = [arena.tile([P, T], F32, name="wd_raw%d" % i, align_bytes=DMA_ALIGN, offset=RAW * i) for i in range(4)]
        x_raw = [arena.tile([P, 4, M], F32, name="x_raw%d" % a, align_bytes=DMA_ALIGN, offset=RAW * (4 + a)) for a in range(2)]
        gam_row = keep.tile([P, M], F32, name="gam_row")
        gam_cols = keep.tile([P, 4], F32, name="gam_cols")

        nc.gpsimd.memset(tab_s[:].bitcast(I32), 0)
        nc.vector.memset(xn_s[:].rearrange("p a c -> p (a c)").bitcast(I32), 0)
        nc.vector.memset(v_s1[:].rearrange("p t c -> p (t c)").bitcast(I32), 0)
        make_identity(nc, ident[:])
        nc.scalar.dma_start(g_raw[:], g.rearrange("(b c) -> b c", b=2))
        nc.scalar.activation(rows[:], ident[:].unsqueeze(1).to_broadcast([P, 4, P]), ACT.Copy, scale=0.0)

        nc.sync.dma_start(offsets[:], offs)
        nc.sync.dma_start(xn_w[:].bitcast(I32), xn_words.rearrange("a p c -> p a c").bitcast(I32))
        for r in range(4):
            nc.sync.dma_start(tab_s[r:P:16, :].bitcast(I32), tab_scales[:, r:16:4, :].rearrange("a q c -> q a c").bitcast(I32))
        nc.sync.dma_start(tab_w[0][:].bitcast(I32), tab_words[0].rearrange("p t i -> p (t i)").bitcast(I32))
        nc.sync.dma_start(gam_cols[:], gam.rearrange("(p c) -> p c", c=4))
        nc.sync.dma_start(tab_w[1][:].bitcast(I32), tab_words[1].rearrange("p t i -> p (t i)").bitcast(I32))
        for r in range(4):
            nc.sync.dma_start(xn_s[r:P:32, :, :].bitcast(I32), xn_scales[:, r:16:4, :].rearrange("a q c -> q a c").bitcast(I32))

        nc.vector.tensor_copy(v_s[:].rearrange("p t (c r) -> p c t r", r=8), tab_s[:].indirect(offsets[:]))
        x_rows = [x[512 * a : 512 * (a + 1), :].rearrange("(p j) m -> p j m", j=4) for a in range(2)]
        nc.sync.dma_start(wd_raw[0][:, 0:AHEAD], wdT[0:P, 0:AHEAD])
        nc.sync.dma_start(
            v_s1[0:112, :, :].rearrange("p t c -> p (t c)").bitcast(I32),
            v_s[16:P, :, :].rearrange("p t c -> p (t c)").bitcast(I32),
        )
        nc.sync.dma_start(wd_raw[0][:, AHEAD:T], wdT[0:P, AHEAD:T])
        nc.sync.dma_start(wd_raw[1][:], wdT[P : 2 * P, :])
        nc.sync.dma_start(x_raw[0][:], x_rows[0])
        nc.sync.dma_start(x_raw[1][:], x_rows[1])
        for i in range(2, 4):
            nc.sync.dma_start(wd_raw[i][:], wdT[P * i : P * (i + 1), :])

        nc.vector.tensor_copy(v_w0[:].rearrange("p t (c r) -> p c t r", r=8), tab_w[0][:].indirect(offsets[:]))
        for b in range(2):
            nc.vector.tensor_copy(v_w1[b][:].rearrange("p t (c r) -> p c t r", r=8), tab_w[1][:].indirect(offsets[:, 32 * b : 32 * (b + 1)]))

        nc.scalar.copy(rows[0:2, :, :].rearrange("b t (q r) -> b t q r", r=8), g_raw[:].rearrange("b (q t r) -> b t q r", t=4, r=8))
        cols_ps = psum.tile([P, 4, P], F32, name="cols_ps", tag="bank7")
        for t in range(4):
            nc.tensor.transpose(cols_ps[:, t, :], rows[:, t, :], ident[:])
        g_cols = cols_ps[:, :, 0:2].rearrange("p t b -> p b t")
        gain = keep.tile([P, 2, 4], F32, name="gain")
        sign0 = keep.tile([P, 2, 4], F32, name="sign0")
        sign = keep.tile([P, 2, 4], BF16, name="sign")
        g_odd = keep.tile([P, 2], F32, name="g_odd")
        gain_odd = arena.tile([P, 2], F32, name="gain_odd", align_bytes=64, offset=RAW * 5 + 6144)
        nc.scalar.activation(gain[:, 0, :], g_cols[:, 0, :], ACT.Abs)
        nc.scalar.activation(gain[:, 1, 0:4:2], g_cols[:, 1, 0:4:2], ACT.Abs)
        nc.scalar.copy(g_odd[:], g_cols[:, 1, 1:4:2])

        def gain_of(b, t):
            return gain_odd[:, t // 2 : t // 2 + 1] if b == 1 and t % 2 == 1 else gain[:, b, t : t + 1]

        nc.scalar.activation(sign0[:], g_cols, ACT.Sign)
        nc.scalar.activation(sign[:], sign0[:], ACT.Sign, bias=0.5)

        spread = psum.tile([P, 4, P], F32, name="spread", tag="bank7")
        for c in range(4):
            nc.tensor.transpose(spread[:, c, :], gam_cols[:, c : c + 1].to_broadcast([P, P]), ident[:])
        nc.scalar.copy(gam_row[:].rearrange("p (r c) -> p r c", c=4), spread[:].rearrange("p c r -> p r c"))

        x_w = [keep.tile([P, M], U32, name="x_w%d" % a, align_bytes=64) for a in range(2)]
        x_s = [keep.tile([P, M], U8, name="x_s%d" % a, align_bytes=64) for a in range(2)]
        x_bf = [arena.tile([P, M, 4], BF16, name="x_bf%d" % a, align_bytes=64, offset=ROUNDED_X[a]) for a in range(2)]

        def round_x(copy, a, lo, hi):
            cols = slice(lo, hi)
            copy(
                x_bf[a][:, cols, :].rearrange("p (c i) t -> p c t i", i=4),
                x_raw[a][:, :, cols].rearrange("p t (c i) -> p c t i", i=4),
            )

        def quantise_x(a):
            nc.vector.quantize_mx(x_w[a][:].bitcast(FP8X4), x_s[a][:], x_bf[a][:].rearrange("p c t -> p (c t)"))

        h_w, h_s, h_bf, h_pairs, sums = {}, {}, {}, {}, {}

        def hidden(side, b, codes=(0, 2, 1, 3)):
            for t in codes:
                acc = psum.tile([P, M], F32, name="acc", tag="bank%d" % HIDDEN_BANKS[side][4 * b + t])
                cols = slice(P * b, P * (b + 1))
                early = (b == 0 and t % 2 == 0) if side == "next" else b == 0
                passes = (0, 1) if early else (1, 0)
                for a in passes:
                    words = v_w0[:, t, cols] if a == 0 else v_w1[b][:, t, :]
                    if a == 0:
                        plane = v_s[:, t, cols]
                    else:
                        plane = v_s1[:, t, cols]
                    if side == "next":
                        rhs, rhs_scale = xn_w[:, a, :].bitcast(FP4X4), xn_s[:, a, :]
                    else:
                        rhs, rhs_scale = x_w[a][:].bitcast(FP8X4), x_s[a][:]
                    nc.tensor.matmul_mx(acc[:], words.bitcast(FP8X4), plane, rhs, rhs_scale, start=(a == passes[0]), stop=(a == passes[1]))
                sums[side, b, t] = acc

        def rectify(side, b, codes=(0, 2, 1, 3)):
            if (side, b) not in h_pairs:
                h_pairs[side, b] = arena.tile([P, 2, M, 2], BF16, name="pairs", align_bytes=64, offset=PAIRS)
            for t in codes:
                nc.scalar.activation(h_pairs[side, b][:, t // 2, :, t % 2], sums[side, b, t][:], ACT.Relu, scale=gain_of(b, t))

        def rectify_rows(side, b, codes=(0, 2, 1, 3)):
            if (side, b) not in h_pairs:
                h_pairs[side, b] = arena.tile([P, 4, M], BF16, name="h_rows_%s%d" % (side, b), align_bytes=64, offset=ROWS[side, b])
            for t in codes:
                nc.scalar.activation(h_pairs[side, b][:, t, :], sums[side, b, t][:], ACT.Relu, scale=gain_of(b, t))

        def weave_h(side, b):
            h_bf[side, b] = arena.tile([P, M, 4], BF16, name="h_bf_%s%d" % (side, b), align_bytes=64, offset=ROUNDED_H[side, b])
            nc.gpsimd.tensor_scalar(
                h_bf[side, b][:].rearrange("p (c i) t -> p c t i", i=4),
                h_pairs[side, b][:].rearrange("p t (c i) -> p c t i", i=4),
                1.0, 0.0, ALU.mult, ALU.add,
            )

        def join_h(copy, side, b):
            h_bf[side, b] = arena.tile([P, M, 4], BF16, name="h_bf_%s%d" % (side, b), align_bytes=64, offset=ROUNDED_H[side, b])
            copy(
                h_bf[side, b][:].bitcast(U32),
                h_pairs[side, b][:].bitcast(U32).rearrange("p u m e -> p m (u e)"),
            )

        def quantise_h(side, b, place):
            h_w[side, b] = keep.tile([P, M], U32, name="h_w_%s%d" % (side, b), align_bytes=64)
            if place is None:
                h_s[side, b] = keep.tile([P, M], U8, name="h_s_%s%d" % (side, b), align_bytes=64)
            else:
                h_s[side, b] = arena.tile([P, M], U8, name="h_s_%s%d" % (side, b), align_bytes=64, offset=place)
            nc.vector.quantize_mx(h_w[side, b][:].bitcast(FP8X4), h_s[side, b][:], h_bf[side, b][:].rearrange("p c t -> p (c t)"))

        wd_picked, wd_turned, wd_bf, wd_w, wd_s = {}, {}, {}, {}, {}

        def pick_wd(i, place):
            picked = arena.tile([P, 2, 2 * P, 2], BF16, name="picked%d" % i, align_bytes=64, offset=place)
            wd_picked[i] = picked
            nc.vector.tensor_copy(picked[:].rearrange("p u (c r) e -> p c u e r", r=8), wd_raw[i][:].indirect(offsets[:]))

        def turn_wd(i):
            words = wd_picked[i][:].rearrange("p u c e -> p u (c e)").bitcast(F32)
            turned = psum.tile([P, 2, 2, P], F32, name="turned", tag="bank%d" % TURN_BANKS[i])
            wd_turned[i] = turned
            for b in range(2):
                for u in range(2):
                    nc.tensor.transpose(turned[:, u, b, :], words[:, u, P * b : P * (b + 1)], ident[:])

        def sign_halves(i, place):
            wd_bf[i] = arena.tile([P, 2 * P, 4], BF16, name="wd_bf%d" % i, align_bytes=64, offset=place)
            for b in range(2):
                nc.vector.tensor_tensor(
                    wd_bf[i][:, P * b : P * (b + 1), :].rearrange("p n (u e) -> p n u e", e=2),
                    wd_turned[i, b][:].bitcast(BF16).rearrange("p u (n e) -> p n u e", e=2),
                    sign[:, b, :].rearrange("p (u e) -> p u e", e=2).unsqueeze(1).to_broadcast([P, P, 2, 2]),
                    ALU.mult,
                )

        def pick_and_turn_apart(i):
            for b in range(2):
                wd_turned[i, b] = psum.tile([P, 2, P], F32, name="turned", tag="bank%d" % HALF_TURN_BANKS[i][b])
                picked = arena.tile([P, 2, P, 2], BF16, name="picked%d_%d" % (i, b), align_bytes=64, offset=PICKED_HALVES[i][b])
                nc.vector.tensor_copy(picked[:].rearrange("p u (c r) e -> p c u e r", r=8), wd_raw[i][:].indirect(offsets[:, 32 * b : 32 * (b + 1)]))
                words = picked[:].rearrange("p u c e -> p u (c e)").bitcast(F32)
                for u in range(2):
                    nc.tensor.transpose(wd_turned[i, b][:, u, :], words[:, u, :], ident[:])

        def sign_wd(i, place):
            wd_bf[i] = arena.tile([P, 2 * P, 4], BF16, name="wd_bf%d" % i, align_bytes=64, offset=place)
            nc.vector.tensor_tensor(
                wd_bf[i][:].rearrange("p (b n) (u e) -> p b n u e", b=2, e=2),
                wd_turned[i][:].bitcast(BF16).rearrange("p u b (n e) -> p b n u e", e=2),
                sign[:].rearrange("p b (u e) -> p b u e", e=2).unsqueeze(2).to_broadcast([P, 2, P, 2, 2]),
                ALU.mult,
            )

        def quantise_wd(i, place=None):
            if place is None:
                wd_w[i] = keep.tile([P, 2 * P], U32, name="wd_w%d" % i, align_bytes=64)
            else:
                wd_w[i] = arena.tile([P, 2 * P], U32, name="wd_w%d" % i, align_bytes=64, offset=place)
            wd_s[i] = keep.tile([P, 2 * P], U8, name="wd_s%d" % i, align_bytes=64)
            nc.vector.quantize_mx(wd_w[i][:].bitcast(FP8X4), wd_s[i][:], wd_bf[i][:].rearrange("p c t -> p (c t)"))

        sums_down = {}

        def down(side, i, passes=(0, 1)):
            if (side, i) not in sums_down:
                sums_down[side, i] = psum.tile([P, M], F32, name="y", tag="bank%d" % DOWN_BANKS[side][i])
            y = sums_down[side, i]
            first = 1 if side == "now" and i < 2 else 0
            for b in passes:
                cols_n = slice(P * b, P * (b + 1))
                nc.tensor.matmul_mx(
                    y[:], wd_w[i][:, cols_n].bitcast(FP8X4), wd_s[i][:, cols_n],
                    h_w[side, b][:].bitcast(FP8X4), h_s[side, b][:], start=(b == first), stop=(b != first),
                )
            return y

        discounted = {}
        copied = arena.tile([P, 2, M], F32, name="copied", align_bytes=64, offset=PAIRS - 4096 + 64)

        def discount(i, place):
            late = arena.tile([P, M], F32, name="discounted%d" % i, align_bytes=64, offset=place)
            discounted[i] = late[:]
            nc.vector.tensor_tensor(discounted[i], sums_down["next", i][:], gam_row[:], ALU.mult)

        def discount_aside(i, pieces):
            nc.scalar.copy(copied[:, i, :], sums_down["next", i][:])
            aside = arena.tile([P, M], F32, name="discounted%d" % i, align_bytes=64, offset=ROUNDED_H["now", 1] + 2 * KIB * i)
            discounted[i] = aside[:]
            width = M // pieces
            for piece in range(pieces):
                cols = slice(width * piece, width * (piece + 1))
                nc.gpsimd.tensor_tensor(aside[:, cols], copied[:, i, cols], gam_row[:, cols], ALU.mult)

        def finish(i, pieces=1):
            y = sums_down["now", i]
            width = M // pieces
            for piece in range(pieces):
                cols = slice(width * piece, width * (piece + 1))
                result = keep.tile([P, width], F32, name="result%d_%d" % (i, piece), align_bytes=DMA_ALIGN)
                nc.vector.tensor_tensor(result[:], discounted[i][:, cols], y[:, cols], ALU.subtract)
                nc.sync.dma_start(out[P * i : P * (i + 1), cols], result[:])

        hidden("next", 0)
        rectify_rows("next", 0)
        hidden("next", 1, (0, 2))
        rectify_rows("next", 1, (0, 2))
        weave_h("next", 0)
        pick_wd(0, 84 * KIB)
        turn_wd(0)
        pick_and_turn_apart(1)
        sign_wd(0, PICKED_HALVES[1][0])
        sign_halves(1, ROUNDED_H["next", 1])
        quantise_h("next", 0, None)
        hidden("next", 1, (1, 3))
        round_x(nc.scalar.copy, 0, 0, M)
        quantise_wd(0, ROWS["next", 0] + 2 * KIB)
        quantise_x(0)
        round_x(nc.vector.tensor_copy, 1, 5 * M // 8, M)
        round_x(nc.scalar.copy, 1, 0, M // 2)
        round_x(nc.scalar.copy, 1, M // 2, 5 * M // 8)
        for half in range(2):
            lo, hi = M // 2 * half, M // 2 * (half + 1)
            nc.vector.quantize_mx(x_w[1][:, lo:hi].bitcast(FP8X4), x_s[1][:, lo:hi], x_bf[1][:, lo:hi, :].rearrange("p c t -> p (c t)"))
        nc.scalar.activation(gain_odd[:], g_odd[:], ACT.Abs)
        rectify_rows("next", 1, (1, 3))
        quantise_wd(1, RAW * 5)
        weave_h("next", 1)
        hidden("now", 0)
        hidden("now", 1, (0, 2))
        rectify_rows("now", 0)
        hidden("now", 1, (1, 3))
        weave_h("now", 0)
        rectify("now", 1)
        join_h(nc.scalar.copy, "now", 1)
        pick_wd(2, ROUNDED_X[1])
        turn_wd(2)
        for i in range(2):
            down("next", i, (0,))
        pick_and_turn_apart(3)
        sign_wd(2, PICKED_HALVES[3][0] - 2048 + 64)
        sign_halves(3, SIGNED_LAST)
        quantise_h("next", 1, ROWS["now", 0])
        quantise_wd(2, ROWS["now", 0] + KIB)
        quantise_h("now", 0, None)
        quantise_wd(3, ROWS["now", 0] + 2 * KIB)
        quantise_h("now", 1, None)
        for i in range(2):
            down("next", i, (1,))
        down("next", 2)
        down("now", 2, (0,))
        down("next", 3)
        down("now", 2, (1,))
        down("now", 3)
        for i in range(2):
            down("now", i, (1, 0))
        for i in range(2):
            discount_aside(i, i + 1)
        discount(2, PAIRS + 4096 - 64)
        discount(3, PAIRS + 64)
        for i in (2, 3, 0):
            finish(i)
        finish(1, 2)
